import numpy as np
import ml_dtypes


def mxq(x, axis, fmt="e4m3"):
    dtype, down = {"e4m3": (ml_dtypes.float8_e4m3fn, 7), "e5m2": (ml_dtypes.float8_e5m2, 14)}[fmt]
    v = np.moveaxis(np.asarray(x, np.float32).astype(ml_dtypes.bfloat16).astype(np.float64), axis, -1)
    blocks = v.reshape(v.shape[:-1] + (-1, 32))
    amax = np.abs(blocks).max(-1, keepdims=True)
    byte = np.maximum(np.where(amax > 0, np.frexp(amax)[1] - 1 + 127, 0) - down, 1)
    scale = np.exp2(byte - 127.0)
    codes = (blocks / scale).astype(np.float32).astype(dtype).astype(np.float64)
    return np.moveaxis((codes * scale).reshape(v.shape), -1, axis)


WIDE = False


def mx_kscale(k):
    if not WIDE:
        return np.ones(k)
    levels = np.array([10, -10, 5, -5, 0])
    if k % 512:
        return np.exp2(np.random.permutation(np.resize(levels, k // 32))).repeat(32)
    a = np.empty((k // 512, 16))
    for p in range(k // 512):
        a[p, :8] = np.random.permutation(np.resize(levels, 8))
        for g in range(8):
            far = levels[np.abs(levels - a[p, g]) >= 10]
            a[p, g + 8] = far[np.random.randint(len(far))]
    return np.exp2(a.ravel()).repeat(32)


def f64(x):
    return np.asarray(x).astype(np.float64)


def striped(idx):
    return np.tile(idx.reshape(-1, 16).T, (8, 1)).astype(np.uint16)


def unstriped(offs):
    return offs[:16].T.reshape(-1).astype(np.int64)


E2M1 = np.array([0.0, 0.5, 1.0, 1.5, 2.0, 3.0, 4.0, 6.0, -0.0, -0.5, -1.0, -1.5, -2.0, -3.0, -4.0, -6.0])


def pack_weight(w, fmt):
    k, n = w.shape
    w = f64(np.asarray(w, np.float32).astype(ml_dtypes.bfloat16)).reshape(k // 32, 32, n)
    amax = np.abs(w).max(1)
    if fmt == "e4m3":
        byte = np.frexp(amax)[1] - 1 + 127 - 7
    else:
        mant, ex = np.frexp(amax / 6.0)
        byte = np.where(mant > 0.5, ex, ex - 1) + 127
    byte = np.clip(np.where(amax > 0, byte, 1), 1, 254)
    scaled = (w * np.exp2(127.0 - byte)[:, None, :]).reshape(k, n).astype(np.float32)
    by_word = np.ascontiguousarray(scaled.reshape(k // 512, 128, 4, n).transpose(0, 1, 3, 2))
    if fmt == "e4m3":
        words = by_word.astype(ml_dtypes.float8_e4m3fn).view(np.uint8)
    else:
        c = by_word.astype(ml_dtypes.float4_e2m1fn).view(np.uint8) & 0xF
        words = (c[..., 0::2] | (c[..., 1::2] << 4)).reshape(k // 512, 128, 2 * n)
    return np.ascontiguousarray(words), np.ascontiguousarray(byte.astype(np.uint8).reshape(k // 512, 16, n))


def unpack_weight(words, scales, fmt):
    g, _, n = scales.shape
    words = np.ascontiguousarray(words).reshape(g, 128, n, -1)
    if fmt == "e4m3":
        vals = words.view(ml_dtypes.float8_e4m3fn).astype(np.float64)
    else:
        nib = np.empty((g, 128, n, 4), np.uint8)
        nib[..., 0::2] = words & 0xF
        nib[..., 1::2] = words >> 4
        vals = E2M1[nib]
    vals = vals * np.repeat(np.exp2(scales.astype(np.float64) - 127.0), 8, axis=1)[..., None]
    return vals.transpose(0, 1, 3, 2).reshape(g * 512, n)


def gelu(v):
    return 0.5 * v * (1.0 + np.tanh(np.sqrt(2.0 / np.pi) * (v + 0.044715 * v**3)))


K, T, S, H, N = 512, 2048, 1024, 1024, 512

def setup_inputs():
    n = np.random.standard_normal
    s = mx_kscale(K)[:, None]
    u = mx_kscale(H)[:, None]
    tab_words, tab_scales = pack_weight(n((K, T)) * s, "e4m3")
    wa_words, wa_scales = pack_weight(n((K, H)) / np.sqrt(K) / s * u.T, "e2m1")
    wb_words, wb_scales = pack_weight(n((K, H)) / np.sqrt(K) / s * u.T, "e4m3")
    return {
        "tab_words": tab_words, "tab_scales": tab_scales,
        "offs": striped(np.random.permutation(T)[:S]),
        "offs2": striped(np.random.permutation(T)[:S]),
        "offs3": striped(np.random.permutation(T)[:S]),
        "wc": (n((K, H)) / np.sqrt(K) / s * u.T).astype(np.float32),
        "wa_words": wa_words, "wa_scales": wa_scales,
        "wb_words": wb_words, "wb_scales": wb_scales,
        "wo": (n((H, N)) / np.sqrt(H) / u).astype(np.float32),
        "bo": (0.5 * n(N)).astype(np.float32),
    }

def reference(tab_words, tab_scales, offs, offs2, offs3, wc, wa_words, wa_scales, wb_words, wb_scales, wo, bo):
    v = unpack_weight(tab_words, tab_scales, "e4m3")
    vc = v[:, unstriped(offs)]
    va = v[:, unstriped(offs2)]
    vb = v[:, unstriped(offs3)]
    wa = unpack_weight(wa_words, wa_scales, "e2m1")
    wb = unpack_weight(wb_words, wb_scales, "e4m3")
    c = mxq(f64(wc), 0, "e4m3").T @ vc
    a = wa.T @ va
    b = wb.T @ vb
    h = np.maximum(np.maximum(a, b) - c, 0.0)
    y = mxq(f64(wo), 0, "e4m3").T @ mxq(h, 0, "e4m3")
    return np.maximum(y + f64(bo)[:, None], 0.0)

@@ -1,0 +1,232 @@
+from contextlib import ExitStack
+
+import concourse.mybir as mybir
+
+K, T, S, H, N = 512, 2048, 1024, 1024, 512
+FLOPS = 2 * (3 * K * H * S + H * N * S)
+
+F32 = mybir.dt.float32
+BF16 = mybir.dt.bfloat16
+I32 = mybir.dt.int32
+U32 = mybir.dt.uint32
+U16 = mybir.dt.uint16
+U8 = mybir.dt.uint8
+FP8X4 = mybir.dt.float8_e4m3fn_x4
+FP4X4 = mybir.dt.float4_e2m1fn_x4
+ACT = mybir.ActivationFunctionType
+ALU = mybir.AluOpType
+
+P = 128
+J = 128
+UNITS = 16
+TWICE = (3, 6, 7, 11, 14, 15)
+ORDER = [(2 * g + part, b) for g in range(3) for b in range(2) for part in range(2)] + [(6, 0), (6, 1), (7, 0), (7, 1)]
+GATHER = 256
+OUT_BLOCKS = ((0, 256), (256, 256), (512, 256), (768, 128), (896, 128))
+
+
+def tile_list_point_edge_conv_kernel(tc, tab_words, tab_scales, offs, offs2, offs3, wc, wa_words, wa_scales,
+                                               wb_words, wb_scales, wo, bo, out):
+    nc = tc.nc
+    with ExitStack() as ctx:
+        keep = ctx.enter_context(tc.tile_pool(name="keep", bufs=1))
+        ring = ctx.enter_context(tc.tile_pool(name="ring", bufs=4))
+        picked = ctx.enter_context(tc.tile_pool(name="picked", bufs=2))
+        psum1 = ctx.enter_context(tc.psum_pool(name="psum1", bufs=6))
+        psum2 = ctx.enter_context(tc.psum_pool(name="psum2", bufs=2))
+
+        lists = [keep.tile([P, S // 16], U16, name="list%d" % i) for i in range(3)]
+        tab_w = keep.tile([P, T], I32, align_bytes=64)
+        tab_s = keep.tile([P, T // 4], I32, align_bytes=64)
+        got_w, got_s = {}, {}
+        wc_raw = [keep.tile([P, 4, 512], F32, name="wc_raw%d" % b) for b in range(2)]
+        wc_bf = [keep.tile([P, 2048], BF16, name="wc_bf%d" % b, align_bytes=64) for b in range(2)]
+        wc_q = keep.tile([P, H], U32, align_bytes=64)
+        wc_s = keep.tile([P, H], U8, align_bytes=64)
+        wa_raw = keep.tile([P, H // 2], I32, align_bytes=64)
+        wa_q = keep.tile([P, H // 2], I32, align_bytes=64)
+        wb_raw = keep.tile([P, H], I32, align_bytes=64)
+        wb_q = keep.tile([P, H], I32, align_bytes=64)
+        ws_raw = keep.tile([P, 2, H // 4], I32, align_bytes=64)
+        ws = keep.tile([P, 2, H // 4], I32, align_bytes=64)
+        wo_raw = [keep.tile([P, 4, N], F32, name="wo_raw%d" % b) for b in range(2)]
+        wo_bf = [keep.tile([P, 4 * N], BF16, name="wo_bf%d" % b, align_bytes=64) for b in range(2)]
+        wo_q = keep.tile([P, 2, N], U32, align_bytes=64)
+        wo_s = keep.tile([P, 2, N], U8, align_bytes=64)
+        bias = keep.tile([P, 4], F32)
+        h_bf = keep.tile([P, 2 * S * 4], BF16, align_bytes=64)
+        h_q = keep.tile([P, 2 * S], U32, align_bytes=64)
+        h_s = keep.tile([P, 2 * S], U8, align_bytes=64)
+        res = keep.tile([P, 4, S], F32)
+
+        def load_scales(dst, src):
+            for q in range(4):
+                nc.sync.dma_start(dst[32 * q : 32 * q + 4, :], src[0, 4 * q : 4 * q + 4, :].bitcast(I32))
+
+        nc.vector.memset(tab_s[:], 0)
+        nc.vector.memset(ws_raw[:], 0)
+        wc_rows = wc.rearrange("(p i) r -> p i r", i=4)
+        nc.sync.dma_start(lists[0][:], offs)
+        load_scales(tab_s, tab_scales)
+        nc.sync.dma_start(tab_w[:], tab_words[0].rearrange("p t i -> p (t i)").bitcast(I32))
+        nc.sync.dma_start(wc_raw[0][:], wc_rows[:, :, 0:512])
+        nc.sync.dma_start(lists[1][:], offs2)
+        nc.sync.dma_start(lists[2][:], offs3)
+        load_scales(ws_raw[:, 0, :], wa_scales)
+        nc.sync.dma_start(wb_raw[:], wb_words[0].rearrange("p e i -> p (e i)").bitcast(I32))
+        nc.sync.dma_start(wa_raw[:], wa_words[0].bitcast(I32))
+        load_scales(ws_raw[:, 1, :], wb_scales)
+        nc.sync.dma_start(wc_raw[1][:], wc_rows[:, :, 512:1024])
+        wo_rows = wo.rearrange("(b u t s) n -> b t u s n", b=2, t=4, s=4)
+        for b in range(2):
+            for t in range(4):
+                nc.sync.dma_start(wo_raw[b][:, t, :], wo_rows[b, t])
+        with nc.allow_non_contiguous_dma(reason="one bias value a partition"):
+            nc.sync.dma_start(bias[:], bo.rearrange("(t p) -> p t", p=P))
+
+        def offsets(i, g):
+            return lists[i][:, g * GATHER // 16 : (g + 1) * GATHER // 16]
+
+        def gather_words(g):
+            for i in range(3):
+                words = picked.tile([P, GATHER], U32, name="words%d" % i, align_bytes=64)
+                nc.vector.tensor_copy(words[:], tab_w[:].bitcast(U32).indirect(offsets(i, g)))
+                got_w.setdefault((i, g), words)
+
+        def gather_scales(g):
+            for i in range(3):
+                scales = picked.tile([P, GATHER], U8, name="scales%d" % i, align_bytes=64)
+                nc.vector.tensor_copy(scales[:], tab_s[:].bitcast(U8).indirect(offsets(i, g)))
+                got_s.setdefault((i, g), scales)
+
+        def quantize_wc(b):
+            src = wc_raw[b][:].rearrange("p i (u t s) -> p t u i s", t=4, s=4)
+            dst = wc_bf[b][:].rearrange("p (t u s i) -> p t u i s", t=4, s=4, i=4)
+            for t in range(4):
+                nc.scalar.activation(dst[:, t], src[:, t], ACT.Copy, scale=-1.0)
+            nc.vector.quantize_mx(out=wc_q[:, 512 * b : 512 * (b + 1)].bitcast(FP8X4), scales=wc_s[:, 512 * b : 512 * (b + 1)],
+                                  in_=wc_bf[b][:])
+
+        gather_scales(0)
+        gather_words(0)
+        quantize_wc(0)
+        nc.vector.tensor_copy(wb_q[:].rearrange("p (b t u s) -> p b t u s", b=2, t=4, s=4),
+                              wb_raw[:].rearrange("p (b u t s) -> p b t u s", b=2, t=4, s=4))
+        nc.vector.tensor_copy(wa_q[:].rearrange("p (b t u s) -> p b t u s", b=2, t=4, s=2),
+                              wa_raw[:].rearrange("p (b u t s) -> p b t u s", b=2, t=4, s=2))
+        nc.vector.tensor_copy(ws[:].rearrange("p w (b t u) -> p (w b) t u", b=2, t=4),
+                              ws_raw[:].rearrange("p w (b u t) -> p (w b) t u", b=2, t=4))
+
+        def quantize_wo(b):
+            src = wo_raw[b][:].rearrange("p t (c s) -> p c t s", s=4)
+            dst = wo_bf[b][:].rearrange("p (c s t) -> p c t s", s=4, t=4)
+            for half in range(2):
+                cols = slice(64 * half, 64 * (half + 1))
+                nc.scalar.activation(dst[:, cols], src[:, cols], ACT.Copy)
+            nc.vector.quantize_mx(out=wo_q[:, b, :].bitcast(FP8X4), scales=wo_s[:, b, :], in_=wo_bf[b][:])
+
+        ws_bytes = ws[:].rearrange("p w c -> p (w c)").bitcast(U8)
+
+        def weights(i, col):
+            if i == 0:
+                return wc_q[:, col : col + P].bitcast(FP8X4), wc_s[:, col : col + P]
+            if i == 1:
+                return wa_q[:].bitcast(U8)[:, 2 * col : 2 * (col + P)].bitcast(FP4X4), ws_bytes[:, col : col + P]
+            return wb_q[:, col : col + P].bitcast(FP8X4), ws_bytes[:, H + col : H + col + P]
+
+        def product(bank, i, unit, t, start, stop):
+            jb, b = ORDER[unit]
+            codes, scales = weights(i, 512 * b + P * t)
+            g, part = divmod(jb, GATHER // J)
+            cols = slice(J * part, J * (part + 1))
+            nc.tensor.matmul_mx(out=bank[:, t, :], lhsT=codes, lhsT_scale=scales, rhs=got_w[i, g][:, cols].bitcast(FP8X4),
+                                rhs_scale=got_s[i, g][:, cols], start=start, stop=stop)
+
+        def words_order(bank):
+            return bank[:].rearrange("p t j -> p j t")
+
+        def h_slice(unit):
+            return h_bf[:, 4 * J * unit : 4 * J * (unit + 1)]
+
+        def as_words(ap):
+            return ap.rearrange("p (j t) -> p j t", t=4)
+
+        sides, largers = {}, {}
+
+        def fill_bank(i, unit):
+            bank = psum1.tile([P, 4, J], F32, name="bank")
+            for t in range(4):
+                if unit in TWICE:
+                    product(bank, 0, unit, t, True, False)
+                product(bank, i, unit, t, unit not in TWICE, True)
+            return words_order(bank)
+
+        def stage_b(unit):
+            bank = fill_bank(2, unit)
+            side = ring.tile([P, 4 * J], F32, name="side")
+            nc.scalar.activation(as_words(side[:]), bank, ACT.Relu if unit in TWICE else ACT.Copy)
+            sides.setdefault(unit, side)
+
+        def stage_a(unit):
+            bank = fill_bank(1, unit)
+            if unit in TWICE:
+                nc.vector.tensor_tensor(as_words(h_slice(unit)), bank, as_words(sides[unit][:]), ALU.max)
+            else:
+                larger = ring.tile([P, 4 * J], F32, name="larger")
+                nc.vector.tensor_tensor(as_words(larger[:]), bank, as_words(sides[unit][:]), ALU.max)
+                largers.setdefault(unit, larger)
+
+        def stage_c(unit):
+            if unit not in TWICE:
+                bank = fill_bank(0, unit)
+                nc.vector.tensor_tensor(as_words(h_slice(unit)), bank, as_words(largers[unit][:]), ALU.add)
+
+        def relu_block(j0, width):
+            units = [unit for unit in range(2 * j0 // J, 2 * (j0 + width) // J) if unit not in TWICE]
+            if units:
+                run = h_bf[:, 4 * J * units[0] : 4 * J * (units[-1] + 1)]
+                nc.vector.tensor_scalar_max(run, run, 0.0)
+
+        def quantize_block(j0, width):
+            step = J if j0 + width == S else 2 * width
+            for c0 in range(2 * j0, 2 * (j0 + width), step):
+                nc.vector.quantize_mx(out=h_q[:, c0 : c0 + step].bitcast(FP8X4), scales=h_s[:, c0 : c0 + step],
+                                      in_=h_bf[:, 4 * c0 : 4 * (c0 + step)])
+
+        out_rows = out.rearrange("(t p) j -> p t j", p=P)
+
+        def output_block(j0, width):
+            cols = slice(j0, j0 + width)
+            for pair in range(2):
+                bank = psum2.tile([P, 2, 256], F32, name="ybank")
+                for e in range(2):
+                    nt = 2 * pair + e
+                    for b in range(2):
+                        h_cols = slice(2 * j0 + b * width, 2 * j0 + (b + 1) * width)
+                        nc.tensor.matmul_mx(out=bank[:, e, 0:width], lhsT=wo_q[:, b, P * nt : P * (nt + 1)].bitcast(FP8X4),
+                                            lhsT_scale=wo_s[:, b, P * nt : P * (nt + 1)], rhs=h_q[:, h_cols].bitcast(FP8X4),
+                                            rhs_scale=h_s[:, h_cols], start=(b == 0), stop=(b == 1))
+                for e in range(2):
+                    nt = 2 * pair + e
+                    if pair == 1 and j0 + width == S:
+                        nc.vector.tensor_scalar(res[:, nt, cols], bank[:, e, 0:width], bias[:, nt : nt + 1], 0.0, ALU.add, ALU.max)
+                    else:
+                        nc.scalar.activation(res[:, nt, cols], bank[:, e, 0:width], ACT.Relu, bias=bias[:, nt : nt + 1])
+            nc.sync.dma_start(out_rows[:, :, cols], res[:, :, cols])
+
+        last_unit = {(j0 + width) // J * 2 - 1: (j0, width) for j0, width in OUT_BLOCKS}
+        for step in range(UNITS + 6):
+            for lag, stage in enumerate((stage_b, stage_a, stage_c)):
+                if 0 <= step - lag < UNITS:
+                    stage(step - lag)
+            if step == 0:
+                quantize_wc(1)
+            if step % 4 == 1 and step // 4 + 1 < S // GATHER:
+                gather_scales(step // 4 + 1)
+            if step % 4 == 2 and step // 4 + 1 < S // GATHER:
+                gather_words(step // 4 + 1)
+            if step in (4, 6):
+                quantize_wo(step // 2 - 2)
+            for lag, stage in ((3, relu_block), (4, quantize_block), (5, output_block)):
+                if step - lag in last_unit:
+                    stage(*last_unit[step - lag])

@@ -19,10 +19,23 @@ ALU = mybir.AluOpType
 P = 128
 J = 128
 UNITS = 16
-TWICE = (3, 6, 7, 11, 14, 15)
-ORDER = [(2 * g + part, b) for g in range(3) for b in range(2) for part in range(2)] + [(6, 0), (6, 1), (7, 0), (7, 1)]
-GATHER = 256
-OUT_BLOCKS = ((0, 256), (256, 256), (512, 256), (768, 128), (896, 128))
+TWICE = (2,3,4,5,10,11,)
+TURNED = ()
+ORDER = ((0,0,),(1,0,),(0,1,),(1,1,),(2,0,),(3,0,),(2,1,),(3,1,),(4,0,),(5,0,),(4,1,),(5,1,),(6,0,),(6,1,),(7,0,),(7,1,),)
+RELU_ON_VECTOR = (2,3,5,10,14,15,)
+OUT_BLOCKS = ((0,256,),(256,256,),(512,256,),(768,128,),(896,128,),)
+GATHERS = (
+    ("s", 0, 0, 1024, "head", None),
+    ("s", 1, 0, 1024, "head", None),
+    ("s", 2, 0, 1024, "head", None),
+    ("w", 0, 0, 512, "head", None),
+    ("w", 1, 0, 512, "head", None),
+    ("w", 2, 0, 512, "head", None),
+    ("w", 0, 512, 512, 0, 8192),
+    ("w", 1, 512, 512, 5, 10240),
+    ("w", 2, 512, 512, "weights", 0),
+)
+SIDE_AT = {0: 8192, 5: 10240}
 
 
 def tile_list_point_edge_conv_kernel(tc, tab_words, tab_scales, offs, offs2, offs3, wc, wa_words, wa_scales,
@@ -30,24 +43,23 @@ def tile_list_point_edge_conv_kernel(tc, tab_words, tab_scales, offs, offs2, off
     nc = tc.nc
     with ExitStack() as ctx:
         keep = ctx.enter_context(tc.tile_pool(name="keep", bufs=1))
-        ring = ctx.enter_context(tc.tile_pool(name="ring", bufs=4))
-        picked = ctx.enter_context(tc.tile_pool(name="picked", bufs=2))
+        shared = ctx.enter_context(tc.tile_pool(name="shared", bufs=1))
         psum1 = ctx.enter_context(tc.psum_pool(name="psum1", bufs=6))
         psum2 = ctx.enter_context(tc.psum_pool(name="psum2", bufs=2))
 
         lists = [keep.tile([P, S // 16], U16, name="list%d" % i) for i in range(3)]
         tab_w = keep.tile([P, T], I32, align_bytes=64)
         tab_s = keep.tile([P, T // 4], I32, align_bytes=64)
-        got_w, got_s = {}, {}
+        got = {}
         wc_raw = [keep.tile([P, 4, 512], F32, name="wc_raw%d" % b) for b in range(2)]
         wc_bf = [keep.tile([P, 2048], BF16, name="wc_bf%d" % b, align_bytes=64) for b in range(2)]
         wc_q = keep.tile([P, H], U32, align_bytes=64)
         wc_s = keep.tile([P, H], U8, align_bytes=64)
-        wa_raw = keep.tile([P, H // 2], I32, align_bytes=64)
+        wb_raw = shared.tile([P, H], I32, align_bytes=64, offset=0)
+        wa_raw = shared.tile([P, H // 2], I32, align_bytes=64, offset=4096)
+        ws_raw = shared.tile([P, 2, H // 4], I32, align_bytes=64, offset=6144)
         wa_q = keep.tile([P, H // 2], I32, align_bytes=64)
-        wb_raw = keep.tile([P, H], I32, align_bytes=64)
         wb_q = keep.tile([P, H], I32, align_bytes=64)
-        ws_raw = keep.tile([P, 2, H // 4], I32, align_bytes=64)
         ws = keep.tile([P, 2, H // 4], I32, align_bytes=64)
         wo_raw = [keep.tile([P, 4, N], F32, name="wo_raw%d" % b) for b in range(2)]
         wo_bf = [keep.tile([P, 4 * N], BF16, name="wo_bf%d" % b, align_bytes=64) for b in range(2)]
@@ -63,41 +75,43 @@ def tile_list_point_edge_conv_kernel(tc, tab_words, tab_scales, offs, offs2, off
             for q in range(4):
                 nc.sync.dma_start(dst[32 * q : 32 * q + 4, :], src[0, 4 * q : 4 * q + 4, :].bitcast(I32))
 
+        def load_wo(b):
+            wo_rows = wo.rearrange("(b u t s) n -> b t u s n", b=2, t=4, s=4)
+            for t in range(4):
+                nc.sync.dma_start(wo_raw[b][:, t, :], wo_rows[b, t])
+
         nc.vector.memset(tab_s[:], 0)
         nc.vector.memset(ws_raw[:], 0)
         wc_rows = wc.rearrange("(p i) r -> p i r", i=4)
+        nc.sync.dma_start(wa_raw[:], wa_words[0].bitcast(I32))
         nc.sync.dma_start(lists[0][:], offs)
         load_scales(tab_s, tab_scales)
         nc.sync.dma_start(tab_w[:], tab_words[0].rearrange("p t i -> p (t i)").bitcast(I32))
-        nc.sync.dma_start(wc_raw[0][:], wc_rows[:, :, 0:512])
-        nc.sync.dma_start(lists[1][:], offs2)
-        nc.sync.dma_start(lists[2][:], offs3)
         load_scales(ws_raw[:, 0, :], wa_scales)
-        nc.sync.dma_start(wb_raw[:], wb_words[0].rearrange("p e i -> p (e i)").bitcast(I32))
-        nc.sync.dma_start(wa_raw[:], wa_words[0].bitcast(I32))
-        load_scales(ws_raw[:, 1, :], wb_scales)
+        nc.sync.dma_start(lists[2][:], offs3)
         nc.sync.dma_start(wc_raw[1][:], wc_rows[:, :, 512:1024])
-        wo_rows = wo.rearrange("(b u t s) n -> b t u s n", b=2, t=4, s=4)
-        for b in range(2):
-            for t in range(4):
-                nc.sync.dma_start(wo_raw[b][:, t, :], wo_rows[b, t])
         with nc.allow_non_contiguous_dma(reason="one bias value a partition"):
             nc.sync.dma_start(bias[:], bo.rearrange("(t p) -> p t", p=P))
+        nc.sync.dma_start(lists[1][:], offs2)
+        load_wo(1)
+        load_scales(ws_raw[:, 1, :], wb_scales)
+        nc.sync.dma_start(wc_raw[0][:], wc_rows[:, :, 0:512])
+        nc.sync.dma_start(wb_raw[:], wb_words[0].rearrange("p e i -> p (e i)").bitcast(I32))
+        load_wo(0)
 
-        def offsets(i, g):
-            return lists[i][:, g * GATHER // 16 : (g + 1) * GATHER // 16]
-
-        def gather_words(g):
-            for i in range(3):
-                words = picked.tile([P, GATHER], U32, name="words%d" % i, align_bytes=64)
-                nc.vector.tensor_copy(words[:], tab_w[:].bitcast(U32).indirect(offsets(i, g)))
-                got_w.setdefault((i, g), words)
-
-        def gather_scales(g):
-            for i in range(3):
-                scales = picked.tile([P, GATHER], U8, name="scales%d" % i, align_bytes=64)
-                nc.vector.tensor_copy(scales[:], tab_s[:].bitcast(U8).indirect(offsets(i, g)))
-                got_s.setdefault((i, g), scales)
+        def gather(when):
+            for kind, i, first, count, after, at in GATHERS:
+                if after != when:
+                    continue
+                dtype, window = (U32, tab_w) if kind == "w" else (U8, tab_s)
+                name = "got_%s%d_%d" % (kind, i, first)
+                if at is None:
+                    dst = keep.tile([P, count], dtype, name=name, align_bytes=64)
+                else:
+                    dst = shared.tile([P, count], dtype, name=name, align_bytes=64, offset=at)
+                nc.vector.tensor_copy(dst[:], window[:].bitcast(dtype).indirect(lists[i][:, first // 16 : (first + count) // 16]))
+                for j0 in range(first, first + count, J):
+                    got.setdefault((kind, i, j0 // J), dst[:, j0 - first : j0 - first + J])
 
         def quantize_wc(b):
             src = wc_raw[b][:].rearrange("p i (u t s) -> p t u i s", t=4, s=4)
@@ -107,16 +121,6 @@ def tile_list_point_edge_conv_kernel(tc, tab_words, tab_scales, offs, offs2, off
             nc.vector.quantize_mx(out=wc_q[:, 512 * b : 512 * (b + 1)].bitcast(FP8X4), scales=wc_s[:, 512 * b : 512 * (b + 1)],
                                   in_=wc_bf[b][:])
 
-        gather_scales(0)
-        gather_words(0)
-        quantize_wc(0)
-        nc.vector.tensor_copy(wb_q[:].rearrange("p (b t u s) -> p b t u s", b=2, t=4, s=4),
-                              wb_raw[:].rearrange("p (b u t s) -> p b t u s", b=2, t=4, s=4))
-        nc.vector.tensor_copy(wa_q[:].rearrange("p (b t u s) -> p b t u s", b=2, t=4, s=2),
-                              wa_raw[:].rearrange("p (b u t s) -> p b t u s", b=2, t=4, s=2))
-        nc.vector.tensor_copy(ws[:].rearrange("p w (b t u) -> p (w b) t u", b=2, t=4),
-                              ws_raw[:].rearrange("p w (b u t) -> p (w b) t u", b=2, t=4))
-
         def quantize_wo(b):
             src = wo_raw[b][:].rearrange("p t (c s) -> p c t s", s=4)
             dst = wo_bf[b][:].rearrange("p (c s t) -> p c t s", s=4, t=4)
@@ -125,45 +129,69 @@ def tile_list_point_edge_conv_kernel(tc, tab_words, tab_scales, offs, offs2, off
                 nc.scalar.activation(dst[:, cols], src[:, cols], ACT.Copy)
             nc.vector.quantize_mx(out=wo_q[:, b, :].bitcast(FP8X4), scales=wo_s[:, b, :], in_=wo_bf[b][:])
 
+        gather("head")
+        quantize_wc(0)
+        nc.vector.tensor_copy(wb_q[:].rearrange("p (b t u s) -> p b t u s", b=2, t=4, s=4),
+                              wb_raw[:].rearrange("p (b u t s) -> p b t u s", b=2, t=4, s=4))
+        nc.vector.tensor_copy(wa_q[:].rearrange("p (b t u s) -> p b t u s", b=2, t=4, s=2),
+                              wa_raw[:].rearrange("p (b u t s) -> p b t u s", b=2, t=4, s=2))
+        nc.vector.tensor_copy(ws[:].rearrange("p w (b t u) -> p (w b) t u", b=2, t=4),
+                              ws_raw[:].rearrange("p w (b u t) -> p (w b) t u", b=2, t=4))
+        gather("weights")
+
         ws_bytes = ws[:].rearrange("p w c -> p (w c)").bitcast(U8)
 
-        def weights(i, col):
+        def weights(i, col, count):
             if i == 0:
-                return wc_q[:, col : col + P].bitcast(FP8X4), wc_s[:, col : col + P]
+                return wc_q[:, col : col + count].bitcast(FP8X4), wc_s[:, col : col + count]
             if i == 1:
-                return wa_q[:].bitcast(U8)[:, 2 * col : 2 * (col + P)].bitcast(FP4X4), ws_bytes[:, col : col + P]
-            return wb_q[:, col : col + P].bitcast(FP8X4), ws_bytes[:, H + col : H + col + P]
+                return wa_q[:].bitcast(U8)[:, 2 * col : 2 * (col + count)].bitcast(FP4X4), ws_bytes[:, col : col + count]
+            return wb_q[:, col : col + count].bitcast(FP8X4), ws_bytes[:, H + col : H + col + count]
+
+        def points(i, jb):
+            return got["w", i, jb].bitcast(FP8X4), got["s", i, jb]
 
         def product(bank, i, unit, t, start, stop):
             jb, b = ORDER[unit]
-            codes, scales = weights(i, 512 * b + P * t)
-            g, part = divmod(jb, GATHER // J)
-            cols = slice(J * part, J * (part + 1))
-            nc.tensor.matmul_mx(out=bank[:, t, :], lhsT=codes, lhsT_scale=scales, rhs=got_w[i, g][:, cols].bitcast(FP8X4),
-                                rhs_scale=got_s[i, g][:, cols], start=start, stop=stop)
+            w_codes, w_scales = weights(i, 512 * b + P * t, P)
+            v_codes, v_scales = points(i, jb)
+            nc.tensor.matmul_mx(out=bank[:, t, :], lhsT=w_codes, lhsT_scale=w_scales, rhs=v_codes, rhs_scale=v_scales,
+                                start=start, stop=stop)
 
-        def words_order(bank):
-            return bank[:].rearrange("p t j -> p j t")
+        def h_start(jb, b):
+            j0, width = [blk for blk in OUT_BLOCKS if blk[0] <= J * jb < blk[0] + blk[1]][0]
+            return 2 * j0 + b * width + J * jb - j0
 
         def h_slice(unit):
-            return h_bf[:, 4 * J * unit : 4 * J * (unit + 1)]
+            c0 = h_start(*ORDER[unit])
+            return h_bf[:, 4 * c0 : 4 * (c0 + J)]
 
         def as_words(ap):
             return ap.rearrange("p (j t) -> p j t", t=4)
 
-        sides, largers = {}, {}
+        sides, largers, centres = {}, {}, {}
 
         def fill_bank(i, unit):
             bank = psum1.tile([P, 4, J], F32, name="bank")
+            if unit in TURNED:
+                jb, b = ORDER[unit]
+                w_codes, w_scales = weights(i, 512 * b, 512)
+                v_codes, v_scales = points(i, jb)
+                flat = bank[:].rearrange("p t j -> p (t j)")
+                nc.tensor.matmul_mx(out=flat, lhsT=v_codes, lhsT_scale=v_scales, rhs=w_codes, rhs_scale=w_scales, start=True, stop=True)
+                return as_words(flat)
             for t in range(4):
                 if unit in TWICE:
                     product(bank, 0, unit, t, True, False)
                 product(bank, i, unit, t, unit not in TWICE, True)
-            return words_order(bank)
+            return bank[:].rearrange("p t j -> p j t")
 
         def stage_b(unit):
             bank = fill_bank(2, unit)
-            side = ring.tile([P, 4 * J], F32, name="side")
+            if unit in SIDE_AT:
+                side = shared.tile([P, 4 * J], F32, name="side%d" % unit, align_bytes=64, offset=SIDE_AT[unit])
+            else:
+                side = keep.tile([P, 4 * J], F32, name="side%d" % unit)
             nc.scalar.activation(as_words(side[:]), bank, ACT.Relu if unit in TWICE else ACT.Copy)
             sides.setdefault(unit, side)
 
@@ -172,20 +200,27 @@ def tile_list_point_edge_conv_kernel(tc, tab_words, tab_scales, offs, offs2, off
             if unit in TWICE:
                 nc.vector.tensor_tensor(as_words(h_slice(unit)), bank, as_words(sides[unit][:]), ALU.max)
             else:
-                larger = ring.tile([P, 4 * J], F32, name="larger")
+                larger = keep.tile([P, 4 * J], F32, name="larger%d" % unit)
                 nc.vector.tensor_tensor(as_words(larger[:]), bank, as_words(sides[unit][:]), ALU.max)
                 largers.setdefault(unit, larger)
 
         def stage_c(unit):
-            if unit not in TWICE:
+            if unit in TURNED:
+                bank = fill_bank(0, unit)
+                centre = keep.tile([P, 4 * J], F32, name="centre%d" % unit)
+                nc.scalar.activation(as_words(centre[:]), bank, ACT.Copy)
+                centres.setdefault(unit, centre)
+            elif unit not in TWICE:
                 bank = fill_bank(0, unit)
                 nc.vector.tensor_tensor(as_words(h_slice(unit)), bank, as_words(largers[unit][:]), ALU.add)
 
-        def relu_block(j0, width):
-            units = [unit for unit in range(2 * j0 // J, 2 * (j0 + width) // J) if unit not in TWICE]
-            if units:
-                run = h_bf[:, 4 * J * units[0] : 4 * J * (units[-1] + 1)]
-                nc.vector.tensor_scalar_max(run, run, 0.0)
+        def stage_relu(unit):
+            if unit in TWICE:
+                return
+            elif unit in RELU_ON_VECTOR:
+                nc.vector.tensor_scalar_max(h_slice(unit), h_slice(unit), 0.0)
+            else:
+                nc.scalar.activation(h_slice(unit), h_slice(unit), ACT.Relu)
 
         def quantize_block(j0, width):
             step = J if j0 + width == S else 2 * width
@@ -214,19 +249,17 @@ def tile_list_point_edge_conv_kernel(tc, tab_words, tab_scales, offs, offs2, off
                         nc.scalar.activation(res[:, nt, cols], bank[:, e, 0:width], ACT.Relu, bias=bias[:, nt : nt + 1])
             nc.sync.dma_start(out_rows[:, :, cols], res[:, :, cols])
 
-        last_unit = {(j0 + width) // J * 2 - 1: (j0, width) for j0, width in OUT_BLOCKS}
-        for step in range(UNITS + 6):
-            for lag, stage in enumerate((stage_b, stage_a, stage_c)):
+        last_unit = {max(u for u in range(UNITS) if j0 <= J * ORDER[u][0] < j0 + width): (j0, width) for j0, width in OUT_BLOCKS}
+        for step in range(UNITS + 12):
+            for lag, stage in zip((0,1,2,3,), (stage_b, stage_a, stage_c, stage_relu)):
                 if 0 <= step - lag < UNITS:
                     stage(step - lag)
+            gather(step - 1)
             if step == 0:
                 quantize_wc(1)
-            if step % 4 == 1 and step // 4 + 1 < S // GATHER:
-                gather_scales(step // 4 + 1)
-            if step % 4 == 2 and step // 4 + 1 < S // GATHER:
-                gather_words(step // 4 + 1)
-            if step in (4, 6):
-                quantize_wo(step // 2 - 2)
-            for lag, stage in ((3, relu_block), (4, quantize_block), (5, output_block)):
+            for b, when in enumerate((6,3,)):
+                if step == when:
+                    quantize_wo(b)
+            for lag, stage in ((3, quantize_block), (6, output_block)):
                 if step - lag in last_unit:
                     stage(*last_unit[step - lag])

@@ -18,28 +18,14 @@ ALU = mybir.AluOpType
 
 P = 128
 J = 128
-UNITS = 16
-TWICE = (2,3,4,5,10,11,)
-TURNED = ()
-ORDER = ((0,0,),(1,0,),(0,1,),(1,1,),(2,0,),(3,0,),(2,1,),(3,1,),(4,0,),(5,0,),(4,1,),(5,1,),(6,0,),(6,1,),(7,0,),(7,1,),)
-RELU_ON_VECTOR = (2,3,5,10,14,15,)
-OUT_BLOCKS = ((0,256,),(256,256,),(512,256,),(768,128,),(896,128,),)
-GATHERS = (
-    ("s", 0, 0, 1024, "head", None),
-    ("s", 1, 0, 1024, "head", None),
-    ("s", 2, 0, 1024, "head", None),
-    ("w", 0, 0, 512, "head", None),
-    ("w", 1, 0, 512, "head", None),
-    ("w", 2, 0, 512, "head", None),
-    ("w", 0, 512, 512, 0, 8192),
-    ("w", 1, 512, 512, 5, 10240),
-    ("w", 2, 512, 512, "weights", 0),
-)
-SIDE_AT = {0: 8192, 5: 10240}
+CENTRE, FIRST, SECOND = 0, 1, 2
+OUT_BLOCKS = ((0, 256), (256, 256), (512, 256), (768, 128), (896, 128))
+FOLDED_FROM = 640
+HEAD = 256
 
 
 def tile_list_point_edge_conv_kernel(tc, tab_words, tab_scales, offs, offs2, offs3, wc, wa_words, wa_scales,
-                                               wb_words, wb_scales, wo, bo, out):
+                                                  wb_words, wb_scales, wo, bo, out):
     nc = tc.nc
     with ExitStack() as ctx:
         keep = ctx.enter_context(tc.tile_pool(name="keep", bufs=1))
@@ -50,17 +36,18 @@ def tile_list_point_edge_conv_kernel(tc, tab_words, tab_scales, offs, offs2, off
         lists = [keep.tile([P, S // 16], U16, name="list%d" % i) for i in range(3)]
         tab_w = keep.tile([P, T], I32, align_bytes=64)
         tab_s = keep.tile([P, T // 4], I32, align_bytes=64)
-        got = {}
         wc_raw = [keep.tile([P, 4, 512], F32, name="wc_raw%d" % b) for b in range(2)]
         wc_bf = [keep.tile([P, 2048], BF16, name="wc_bf%d" % b, align_bytes=64) for b in range(2)]
         wc_q = keep.tile([P, H], U32, align_bytes=64)
         wc_s = keep.tile([P, H], U8, align_bytes=64)
-        wb_raw = shared.tile([P, H], I32, align_bytes=64, offset=0)
-        wa_raw = shared.tile([P, H // 2], I32, align_bytes=64, offset=4096)
-        ws_raw = shared.tile([P, 2, H // 4], I32, align_bytes=64, offset=6144)
+        wbs_raw = shared.tile([P, H // 4], I32, align_bytes=64, offset=0)
+        wb_raw = keep.tile([P, H], I32, align_bytes=64)
+        wa_raw = keep.tile([P, H // 2], I32, align_bytes=64)
+        was_raw = shared.tile([P, H // 4], I32, align_bytes=64, offset=5120)
         wa_q = keep.tile([P, H // 2], I32, align_bytes=64)
         wb_q = keep.tile([P, H], I32, align_bytes=64)
-        ws = keep.tile([P, 2, H // 4], I32, align_bytes=64)
+        wa_s = keep.tile([P, H // 4], I32, align_bytes=64)
+        wb_s = keep.tile([P, H // 4], I32, align_bytes=64)
         wo_raw = [keep.tile([P, 4, N], F32, name="wo_raw%d" % b) for b in range(2)]
         wo_bf = [keep.tile([P, 4 * N], BF16, name="wo_bf%d" % b, align_bytes=64) for b in range(2)]
         wo_q = keep.tile([P, 2, N], U32, align_bytes=64)
@@ -80,38 +67,46 @@ def tile_list_point_edge_conv_kernel(tc, tab_words, tab_scales, offs, offs2, off
             for t in range(4):
                 nc.sync.dma_start(wo_raw[b][:, t, :], wo_rows[b, t])
 
-        nc.vector.memset(tab_s[:], 0)
-        nc.vector.memset(ws_raw[:], 0)
+        nc.gpsimd.memset(tab_s[:], 0)
+        nc.gpsimd.memset(wbs_raw[:], 0)
+        nc.gpsimd.memset(was_raw[:], 0)
         wc_rows = wc.rearrange("(p i) r -> p i r", i=4)
         nc.sync.dma_start(wa_raw[:], wa_words[0].bitcast(I32))
-        nc.sync.dma_start(lists[0][:], offs)
+        nc.sync.dma_start(lists[SECOND][:], offs3)
         load_scales(tab_s, tab_scales)
+        nc.sync.dma_start(wb_raw[:], wb_words[0].rearrange("p e i -> p (e i)").bitcast(I32))
         nc.sync.dma_start(tab_w[:], tab_words[0].rearrange("p t i -> p (t i)").bitcast(I32))
-        load_scales(ws_raw[:, 0, :], wa_scales)
-        nc.sync.dma_start(lists[2][:], offs3)
+        load_scales(wbs_raw, wb_scales)
+        nc.sync.dma_start(lists[CENTRE][:], offs)
+        nc.sync.dma_start(wc_raw[0][:], wc_rows[:, :, 0:512])
         nc.sync.dma_start(wc_raw[1][:], wc_rows[:, :, 512:1024])
+        nc.sync.dma_start(lists[FIRST][:], offs2)
+        load_wo(0)
+        load_wo(1)
+        load_scales(was_raw, wa_scales)
         with nc.allow_non_contiguous_dma(reason="one bias value a partition"):
             nc.sync.dma_start(bias[:], bo.rearrange("(t p) -> p t", p=P))
-        nc.sync.dma_start(lists[1][:], offs2)
-        load_wo(1)
-        load_scales(ws_raw[:, 1, :], wb_scales)
-        nc.sync.dma_start(wc_raw[0][:], wc_rows[:, :, 0:512])
-        nc.sync.dma_start(wb_raw[:], wb_words[0].rearrange("p e i -> p (e i)").bitcast(I32))
-        load_wo(0)
 
-        def gather(when):
-            for kind, i, first, count, after, at in GATHERS:
-                if after != when:
-                    continue
-                dtype, window = (U32, tab_w) if kind == "w" else (U8, tab_s)
-                name = "got_%s%d_%d" % (kind, i, first)
-                if at is None:
-                    dst = keep.tile([P, count], dtype, name=name, align_bytes=64)
-                else:
-                    dst = shared.tile([P, count], dtype, name=name, align_bytes=64, offset=at)
-                nc.vector.tensor_copy(dst[:], window[:].bitcast(dtype).indirect(lists[i][:, first // 16 : (first + count) // 16]))
-                for j0 in range(first, first + count, J):
-                    got.setdefault((kind, i, j0 // J), dst[:, j0 - first : j0 - first + J])
+        got = {}
+
+        def gather(window, dtype, i, first, count, dst):
+            nc.vector.tensor_copy(dst[:], window[:].bitcast(dtype).indirect(lists[i][:, first // 16 : (first + count) // 16]))
+            for j0 in range(first, first + count, J):
+                got.setdefault((dtype == U32, i, j0), dst[:, j0 - first : j0 - first + J])
+
+        def gather_scales(i):
+            gather(tab_s, U8, i, 0, S, keep.tile([P, S], U8, name="got_s%d" % i, align_bytes=64))
+
+        def gather_words(i):
+            gather(tab_w, U32, i, 0, S, keep.tile([P, S], U32, name="got_w%d" % i, align_bytes=64))
+
+        def deal_columns(dst, src, run):
+            nc.vector.tensor_copy(dst[:].rearrange("p (b t u s) -> p b t u s", b=2, t=4, s=run),
+                                  src[:].rearrange("p (b u t s) -> p b t u s", b=2, t=4, s=run))
+
+        def deal_scales(dst, src):
+            nc.vector.tensor_copy(dst[:].rearrange("p (b t u) -> p b t u", b=2, t=4),
+                                  src[:].rearrange("p (b u t) -> p b t u", b=2, t=4))
 
         def quantize_wc(b):
             src = wc_raw[b][:].rearrange("p i (u t s) -> p t u i s", t=4, s=4)
@@ -122,104 +117,66 @@ def tile_list_point_edge_conv_kernel(tc, tab_words, tab_scales, offs, offs2, off
                                   in_=wc_bf[b][:])
 
         def quantize_wo(b):
-            src = wo_raw[b][:].rearrange("p t (c s) -> p c t s", s=4)
-            dst = wo_bf[b][:].rearrange("p (c s t) -> p c t s", s=4, t=4)
-            for half in range(2):
-                cols = slice(64 * half, 64 * (half + 1))
-                nc.scalar.activation(dst[:, cols], src[:, cols], ACT.Copy)
+            src = wo_raw[b][:].rearrange("p t n -> p n t")
+            dst = wo_bf[b][:].rearrange("p (n t) -> p n t", t=4)
+            for n0 in range(0, N, P):
+                nc.gpsimd.tensor_scalar(dst[:, n0 : n0 + P], src[:, n0 : n0 + P], 1.0, 0.0, ALU.mult, ALU.add)
             nc.vector.quantize_mx(out=wo_q[:, b, :].bitcast(FP8X4), scales=wo_s[:, b, :], in_=wo_bf[b][:])
 
-        gather("head")
-        quantize_wc(0)
-        nc.vector.tensor_copy(wb_q[:].rearrange("p (b t u s) -> p b t u s", b=2, t=4, s=4),
-                              wb_raw[:].rearrange("p (b u t s) -> p b t u s", b=2, t=4, s=4))
-        nc.vector.tensor_copy(wa_q[:].rearrange("p (b t u s) -> p b t u s", b=2, t=4, s=2),
-                              wa_raw[:].rearrange("p (b u t s) -> p b t u s", b=2, t=4, s=2))
-        nc.vector.tensor_copy(ws[:].rearrange("p w (b t u) -> p (w b) t u", b=2, t=4),
-                              ws_raw[:].rearrange("p w (b u t) -> p (w b) t u", b=2, t=4))
-        gather("weights")
+        def weights(i, col):
+            if i == CENTRE:
+                return wc_q[:, col : col + P].bitcast(FP8X4), wc_s[:, col : col + P]
+            if i == FIRST:
+                return wa_q[:].bitcast(U8)[:, 2 * col : 2 * (col + P)].bitcast(FP4X4), wa_s[:].bitcast(U8)[:, col : col + P]
+            return wb_q[:, col : col + P].bitcast(FP8X4), wb_s[:].bitcast(U8)[:, col : col + P]
 
-        ws_bytes = ws[:].rearrange("p w c -> p (w c)").bitcast(U8)
-
-        def weights(i, col, count):
-            if i == 0:
-                return wc_q[:, col : col + count].bitcast(FP8X4), wc_s[:, col : col + count]
-            if i == 1:
-                return wa_q[:].bitcast(U8)[:, 2 * col : 2 * (col + count)].bitcast(FP4X4), ws_bytes[:, col : col + count]
-            return wb_q[:, col : col + count].bitcast(FP8X4), ws_bytes[:, H + col : H + col + count]
-
-        def points(i, jb):
-            return got["w", i, jb].bitcast(FP8X4), got["s", i, jb]
-
-        def product(bank, i, unit, t, start, stop):
-            jb, b = ORDER[unit]
-            w_codes, w_scales = weights(i, 512 * b + P * t, P)
-            v_codes, v_scales = points(i, jb)
-            nc.tensor.matmul_mx(out=bank[:, t, :], lhsT=w_codes, lhsT_scale=w_scales, rhs=v_codes, rhs_scale=v_scales,
-                                start=start, stop=stop)
-
-        def h_start(jb, b):
-            j0, width = [blk for blk in OUT_BLOCKS if blk[0] <= J * jb < blk[0] + blk[1]][0]
-            return 2 * j0 + b * width + J * jb - j0
+        def fill_bank(terms, unit):
+            j0, b = unit
+            bank = psum1.tile([P, 4, J], F32, name="bank")
+            for t in range(4):
+                for n, i in enumerate(terms):
+                    w_codes, w_scales = weights(i, 512 * b + P * t)
+                    nc.tensor.matmul_mx(out=bank[:, t, :], lhsT=w_codes, lhsT_scale=w_scales, rhs=got[True, i, j0].bitcast(FP8X4),
+                                        rhs_scale=got[False, i, j0], start=(n == 0), stop=(n == len(terms) - 1))
+            return bank[:].rearrange("p t j -> p j t")
 
         def h_slice(unit):
-            c0 = h_start(*ORDER[unit])
+            j0, b = unit
+            first, width = [blk for blk in OUT_BLOCKS if blk[0] <= j0 < blk[0] + blk[1]][0]
+            c0 = 2 * first + b * width + j0 - first
             return h_bf[:, 4 * c0 : 4 * (c0 + J)]
 
         def as_words(ap):
             return ap.rearrange("p (j t) -> p j t", t=4)
 
-        sides, largers, centres = {}, {}, {}
+        units = [(j0, b) for first, width in OUT_BLOCKS for b in range(2) for j0 in range(first, first + width, J)]
+        plain = [u for u in units if u[0] < FOLDED_FROM]
+        folded = [u for u in units if u[0] >= FOLDED_FROM]
+        sides, largers = {}, {}
 
-        def fill_bank(i, unit):
-            bank = psum1.tile([P, 4, J], F32, name="bank")
-            if unit in TURNED:
-                jb, b = ORDER[unit]
-                w_codes, w_scales = weights(i, 512 * b, 512)
-                v_codes, v_scales = points(i, jb)
-                flat = bank[:].rearrange("p t j -> p (t j)")
-                nc.tensor.matmul_mx(out=flat, lhsT=v_codes, lhsT_scale=v_scales, rhs=w_codes, rhs_scale=w_scales, start=True, stop=True)
-                return as_words(flat)
-            for t in range(4):
-                if unit in TWICE:
-                    product(bank, 0, unit, t, True, False)
-                product(bank, i, unit, t, unit not in TWICE, True)
-            return bank[:].rearrange("p t j -> p j t")
-
-        def stage_b(unit):
-            bank = fill_bank(2, unit)
-            if unit in SIDE_AT:
-                side = shared.tile([P, 4 * J], F32, name="side%d" % unit, align_bytes=64, offset=SIDE_AT[unit])
-            else:
-                side = keep.tile([P, 4 * J], F32, name="side%d" % unit)
-            nc.scalar.activation(as_words(side[:]), bank, ACT.Relu if unit in TWICE else ACT.Copy)
+        def stage_side(unit):
+            bank = fill_bank((CENTRE, SECOND) if unit in folded else (SECOND,), unit)
+            side = keep.tile([P, 4 * J], F32, name="side%d_%d" % unit)
+            nc.scalar.activation(as_words(side[:]), bank, ACT.Relu if unit in folded else ACT.Copy)
             sides.setdefault(unit, side)
 
-        def stage_a(unit):
-            bank = fill_bank(1, unit)
-            if unit in TWICE:
+        def stage_max(unit):
+            if unit in folded:
+                bank = fill_bank((CENTRE, FIRST), unit)
                 nc.vector.tensor_tensor(as_words(h_slice(unit)), bank, as_words(sides[unit][:]), ALU.max)
             else:
-                larger = keep.tile([P, 4 * J], F32, name="larger%d" % unit)
+                bank = fill_bank((FIRST,), unit)
+                larger = keep.tile([P, 4 * J], F32, name="larger%d_%d" % unit)
                 nc.vector.tensor_tensor(as_words(larger[:]), bank, as_words(sides[unit][:]), ALU.max)
                 largers.setdefault(unit, larger)
 
-        def stage_c(unit):
-            if unit in TURNED:
-                bank = fill_bank(0, unit)
-                centre = keep.tile([P, 4 * J], F32, name="centre%d" % unit)
-                nc.scalar.activation(as_words(centre[:]), bank, ACT.Copy)
-                centres.setdefault(unit, centre)
-            elif unit not in TWICE:
-                bank = fill_bank(0, unit)
+        def stage_diff(unit):
+            if unit in plain:
+                bank = fill_bank((CENTRE,), unit)
                 nc.vector.tensor_tensor(as_words(h_slice(unit)), bank, as_words(largers[unit][:]), ALU.add)
 
         def stage_relu(unit):
-            if unit in TWICE:
-                return
-            elif unit in RELU_ON_VECTOR:
-                nc.vector.tensor_scalar_max(h_slice(unit), h_slice(unit), 0.0)
-            else:
+            if unit in plain:
                 nc.scalar.activation(h_slice(unit), h_slice(unit), ACT.Relu)
 
         def quantize_block(j0, width):
@@ -233,7 +190,7 @@ def tile_list_point_edge_conv_kernel(tc, tab_words, tab_scales, offs, offs2, off
         def output_block(j0, width):
             cols = slice(j0, j0 + width)
             for pair in range(2):
-                bank = psum2.tile([P, 2, 256], F32, name="ybank")
+                bank = (psum2 if width == 256 else psum1).tile([P, 2, 256], F32, name="bank")
                 for e in range(2):
                     nt = 2 * pair + e
                     for b in range(2):
@@ -249,17 +206,37 @@ def tile_list_point_edge_conv_kernel(tc, tab_words, tab_scales, offs, offs2, off
                         nc.scalar.activation(res[:, nt, cols], bank[:, e, 0:width], ACT.Relu, bias=bias[:, nt : nt + 1])
             nc.sync.dma_start(out_rows[:, :, cols], res[:, :, cols])
 
-        last_unit = {max(u for u in range(UNITS) if j0 <= J * ORDER[u][0] < j0 + width): (j0, width) for j0, width in OUT_BLOCKS}
-        for step in range(UNITS + 12):
-            for lag, stage in zip((0,1,2,3,), (stage_b, stage_a, stage_c, stage_relu)):
-                if 0 <= step - lag < UNITS:
-                    stage(step - lag)
-            gather(step - 1)
-            if step == 0:
-                quantize_wc(1)
-            for b, when in enumerate((6,3,)):
-                if step == when:
-                    quantize_wo(b)
-            for lag, stage in ((3, quantize_block), (6, output_block)):
-                if step - lag in last_unit:
-                    stage(*last_unit[step - lag])
+        deal_columns(wa_q, wa_raw, 2)
+        gather_scales(SECOND)
+        deal_columns(wb_q, wb_raw, 4)
+        gather(tab_w, U32, SECOND, 0, HEAD, keep.tile([P, HEAD], U32, name="got_w2_head", align_bytes=64))
+        deal_scales(wb_s, wbs_raw)
+        gather(tab_w, U32, SECOND, HEAD, S - HEAD, shared.tile([P, S - HEAD], U32, name="got_w2_rest", align_bytes=64, offset=0))
+        gather_scales(CENTRE)
+        gather_words(CENTRE)
+        quantize_wc(0)
+        quantize_wc(1)
+        gather_scales(FIRST)
+        gather(tab_w, U32, FIRST, 0, HEAD, keep.tile([P, HEAD], U32, name="got_w1_head", align_bytes=64))
+        deal_scales(wa_s, was_raw)
+        gather(tab_w, U32, FIRST, HEAD, S - HEAD, shared.tile([P, S - HEAD], U32, name="got_w1_rest", align_bytes=64, offset=5120))
+        for unit in plain + [u for u in folded if u[1] == 0]:
+            stage_side(unit)
+        late_sides = [u for u in folded if u[1] == 1]
+        quantize_wo(0)
+        quantize_wo(1)
+
+        order = plain + folded
+        last_unit = {max(n for n, u in enumerate(order) if j0 <= u[0] < j0 + width): (j0, width) for j0, width in OUT_BLOCKS}
+        for step in range(len(order) + 6):
+            for lag, stage in enumerate((stage_max, stage_diff, stage_relu)):
+                if 0 <= step - lag < len(order):
+                    stage(order[step - lag])
+            if 1 <= step <= len(late_sides):
+                stage_side(late_sides[step - 1])
+            for last, block in last_unit.items():
+                ready = last + (1 if order[last] in folded else 3)
+                if step == ready:
+                    quantize_block(*block)
+                if step == max(ready + 1, len(order) - 1 if block[1] == J else 0):
+                    output_block(*block)

@@ -82,8 +82,8 @@ def tile_list_point_edge_conv_kernel(tc, tab_words, tab_scales, offs, offs2, off
         nc.sync.dma_start(wc_raw[1][:], wc_rows[:, :, 512:1024])
         nc.sync.dma_start(lists[FIRST][:], offs2)
         load_wo(0)
-        load_wo(1)
         load_scales(was_raw, wa_scales)
+        load_wo(1)
         with nc.allow_non_contiguous_dma(reason="one bias value a partition"):
             nc.sync.dma_start(bias[:], bo.rearrange("(t p) -> p t", p=P))
 
@@ -117,10 +117,11 @@ def tile_list_point_edge_conv_kernel(tc, tab_words, tab_scales, offs, offs2, off
                                   in_=wc_bf[b][:])
 
         def quantize_wo(b):
-            src = wo_raw[b][:].rearrange("p t n -> p n t")
-            dst = wo_bf[b][:].rearrange("p (n t) -> p n t", t=4)
-            for n0 in range(0, N, P):
-                nc.gpsimd.tensor_scalar(dst[:, n0 : n0 + P], src[:, n0 : n0 + P], 1.0, 0.0, ALU.mult, ALU.add)
+            src = wo_raw[b][:].rearrange("p t (c s) -> p c t s", s=4)
+            dst = wo_bf[b][:].rearrange("p (c s t) -> p c t s", s=4, t=4)
+            for half in range(2):
+                cols = slice(64 * half, 64 * (half + 1))
+                nc.scalar.activation(dst[:, cols], src[:, cols], ACT.Copy)
             nc.vector.quantize_mx(out=wo_q[:, b, :].bitcast(FP8X4), scales=wo_s[:, b, :], in_=wo_bf[b][:])
 
         def weights(i, col):

@@ -22,6 +22,8 @@ CENTRE, FIRST, SECOND = 0, 1, 2
 OUT_BLOCKS = ((0, 256), (256, 256), (512, 256), (768, 128), (896, 128))
 FOLDED_FROM = 640
 HEAD = 256
+WO_STEPS = (5, 6)
+NARROW = 4
 
 
 def tile_list_point_edge_conv_kernel(tc, tab_words, tab_scales, offs, offs2, offs3, wc, wa_words, wa_scales,
@@ -34,7 +36,7 @@ def tile_list_point_edge_conv_kernel(tc, tab_words, tab_scales, offs, offs2, off
         psum2 = ctx.enter_context(tc.psum_pool(name="psum2", bufs=2))
 
         lists = [keep.tile([P, S // 16], U16, name="list%d" % i) for i in range(3)]
-        tab_w = keep.tile([P, T], I32, align_bytes=64)
+        tab_w = shared.tile([P, T], I32, align_bytes=64, offset=49152)
         tab_s = keep.tile([P, T // 4], I32, align_bytes=64)
         wc_raw = [keep.tile([P, 4, 512], F32, name="wc_raw%d" % b) for b in range(2)]
         wc_bf = [keep.tile([P, 2048], BF16, name="wc_bf%d" % b, align_bytes=64) for b in range(2)]
@@ -49,8 +51,7 @@ def tile_list_point_edge_conv_kernel(tc, tab_words, tab_scales, offs, offs2, off
         wa_s = keep.tile([P, H // 4], I32, align_bytes=64)
         wb_s = keep.tile([P, H // 4], I32, align_bytes=64)
         wo_raw = [keep.tile([P, 4, N], F32, name="wo_raw%d" % b) for b in range(2)]
-        wo_bf = [keep.tile([P, 4 * N], BF16, name="wo_bf%d" % b, align_bytes=64) for b in range(2)]
-        wo_q = keep.tile([P, 2, N], U32, align_bytes=64)
+        wo_bf = [shared.tile([P, 4 * N], BF16, name="wo_bf%d" % b, align_bytes=64, offset=49152 + 4096 * b) for b in range(2)]
         wo_s = keep.tile([P, 2, N], U8, align_bytes=64)
         bias = keep.tile([P, 4], F32)
         h_bf = keep.tile([P, 2 * S * 4], BF16, align_bytes=64)
@@ -116,13 +117,24 @@ def tile_list_point_edge_conv_kernel(tc, tab_words, tab_scales, offs, offs2, off
             nc.vector.quantize_mx(out=wc_q[:, 512 * b : 512 * (b + 1)].bitcast(FP8X4), scales=wc_s[:, 512 * b : 512 * (b + 1)],
                                   in_=wc_bf[b][:])
 
-        def quantize_wo(b):
+        wo_q = []
+
+        def cast_wo_on_gpsimd(b):
+            src = wo_raw[b][:].rearrange("p t n -> p n t")
+            dst = wo_bf[b][:].rearrange("p (n t) -> p n t", t=4)
+            nc.gpsimd.tensor_scalar(dst, src, 1.0, 0.0, ALU.mult, ALU.add)
+
+        def cast_wo_on_scalar(b):
             src = wo_raw[b][:].rearrange("p t (c s) -> p c t s", s=4)
             dst = wo_bf[b][:].rearrange("p (c s t) -> p c t s", s=4, t=4)
             for half in range(2):
                 cols = slice(64 * half, 64 * (half + 1))
                 nc.scalar.activation(dst[:, cols], src[:, cols], ACT.Copy)
-            nc.vector.quantize_mx(out=wo_q[:, b, :].bitcast(FP8X4), scales=wo_s[:, b, :], in_=wo_bf[b][:])
+
+        def quantize_wo(b, after):
+            codes = shared.tile([P, N], U32, name="wo_q%d" % b, align_bytes=64, offset=side_offset(after))
+            nc.vector.quantize_mx(out=codes[:].bitcast(FP8X4), scales=wo_s[:, b, :], in_=wo_bf[b][:])
+            wo_q.append(codes)
 
         def weights(i, col):
             if i == CENTRE:
@@ -153,16 +165,28 @@ def tile_list_point_edge_conv_kernel(tc, tab_words, tab_scales, offs, offs2, off
         units = [(j0, b) for first, width in OUT_BLOCKS for b in range(2) for j0 in range(first, first + width, J)]
         plain = [u for u in units if u[0] < FOLDED_FROM]
         folded = [u for u in units if u[0] >= FOLDED_FROM]
-        sides, largers = {}, {}
+        narrow = folded[:NARROW]
+        sides, largers, others = {}, {}, {}
+
+        def side_offset(unit):
+            return 8192 + 2048 * units.index(unit)
 
         def stage_side(unit):
             bank = fill_bank((CENTRE, SECOND) if unit in folded else (SECOND,), unit)
-            side = keep.tile([P, 4 * J], F32, name="side%d_%d" % unit)
+            side = shared.tile([P, 4 * J], BF16 if unit in narrow else F32, name="side%d_%d" % unit, align_bytes=64, offset=side_offset(unit))
             nc.scalar.activation(as_words(side[:]), bank, ACT.Relu if unit in folded else ACT.Copy)
             sides.setdefault(unit, side)
 
+        def stage_other(unit):
+            bank = fill_bank((CENTRE, FIRST), unit)
+            other = keep.tile([P, 4 * J], BF16, name="other%d_%d" % unit)
+            nc.scalar.activation(as_words(other[:]), bank, ACT.Copy)
+            others.setdefault(unit, other)
+
         def stage_max(unit):
-            if unit in folded:
+            if unit in narrow:
+                nc.vector.tensor_tensor(h_slice(unit), others[unit][:], sides[unit][:], ALU.max)
+            elif unit in folded:
                 bank = fill_bank((CENTRE, FIRST), unit)
                 nc.vector.tensor_tensor(as_words(h_slice(unit)), bank, as_words(sides[unit][:]), ALU.max)
             else:
@@ -188,24 +212,35 @@ def tile_list_point_edge_conv_kernel(tc, tab_words, tab_scales, offs, offs2, off
 
         out_rows = out.rearrange("(t p) j -> p t j", p=P)
 
+        def second_layer(dst, nt, b, j0, width):
+            h_cols = slice(2 * j0 + b * width, 2 * j0 + (b + 1) * width)
+            nc.tensor.matmul_mx(out=dst, lhsT=wo_q[b][:, P * nt : P * (nt + 1)].bitcast(FP8X4), lhsT_scale=wo_s[:, b, P * nt : P * (nt + 1)],
+                                rhs=h_q[:, h_cols].bitcast(FP8X4), rhs_scale=h_s[:, h_cols], start=(b == 0), stop=(b == 1))
+
         def output_block(j0, width):
             cols = slice(j0, j0 + width)
             for pair in range(2):
                 bank = (psum2 if width == 256 else psum1).tile([P, 2, 256], F32, name="bank")
                 for e in range(2):
-                    nt = 2 * pair + e
                     for b in range(2):
-                        h_cols = slice(2 * j0 + b * width, 2 * j0 + (b + 1) * width)
-                        nc.tensor.matmul_mx(out=bank[:, e, 0:width], lhsT=wo_q[:, b, P * nt : P * (nt + 1)].bitcast(FP8X4),
-                                            lhsT_scale=wo_s[:, b, P * nt : P * (nt + 1)], rhs=h_q[:, h_cols].bitcast(FP8X4),
-                                            rhs_scale=h_s[:, h_cols], start=(b == 0), stop=(b == 1))
+                        second_layer(bank[:, e, 0:width], 2 * pair + e, b, j0, width)
                 for e in range(2):
                     nt = 2 * pair + e
-                    if pair == 1 and j0 + width == S:
-                        nc.vector.tensor_scalar(res[:, nt, cols], bank[:, e, 0:width], bias[:, nt : nt + 1], 0.0, ALU.add, ALU.max)
-                    else:
-                        nc.scalar.activation(res[:, nt, cols], bank[:, e, 0:width], ACT.Relu, bias=bias[:, nt : nt + 1])
-            nc.sync.dma_start(out_rows[:, :, cols], res[:, :, cols])
+                    nc.scalar.activation(res[:, nt, cols], bank[:, e, 0:width], ACT.Relu, bias=bias[:, nt : nt + 1])
+                nc.sync.dma_start(out_rows[:, 2 * pair : 2 * pair + 2, cols], res[:, 2 * pair : 2 * pair + 2, cols])
+
+        def output_last_block(j0, width):
+            cols = slice(j0, j0 + width)
+            banks = [psum1.tile([P, 2, 256], F32, name="bank") for nt in range(2)] + [psum2.tile([P, 2, 256], F32, name="bank") for nt in range(2)]
+            for b in range(2):
+                for nt in range(4):
+                    second_layer(banks[nt][:, 0, 0:width], nt, b, j0, width)
+            for nt in range(4):
+                if nt % 2 == 0:
+                    nc.vector.tensor_scalar(res[:, nt, cols], banks[nt][:, 0, 0:width], bias[:, nt : nt + 1], 0.0, ALU.add, ALU.max)
+                else:
+                    nc.scalar.activation(res[:, nt, cols], banks[nt][:, 0, 0:width], ACT.Relu, bias=bias[:, nt : nt + 1])
+                    nc.sync.dma_start(out_rows[:, nt - 1 : nt + 1, cols], res[:, nt - 1 : nt + 1, cols])
 
         deal_columns(wa_q, wa_raw, 2)
         gather_scales(SECOND)
@@ -224,8 +259,8 @@ def tile_list_point_edge_conv_kernel(tc, tab_words, tab_scales, offs, offs2, off
         for unit in plain + [u for u in folded if u[1] == 0]:
             stage_side(unit)
         late_sides = [u for u in folded if u[1] == 1]
-        quantize_wo(0)
-        quantize_wo(1)
+        cast_wo_on_gpsimd(0)
+        cast_wo_on_gpsimd(1)
 
         order = plain + folded
         last_unit = {max(n for n, u in enumerate(order) if j0 <= u[0] < j0 + width): (j0, width) for j0, width in OUT_BLOCKS}
@@ -235,9 +270,14 @@ def tile_list_point_edge_conv_kernel(tc, tab_words, tab_scales, offs, offs2, off
                     stage(order[step - lag])
             if 1 <= step <= len(late_sides):
                 stage_side(late_sides[step - 1])
+            if 0 <= step - 4 < len(narrow):
+                stage_other(narrow[step - 4])
+            for b, when in enumerate(WO_STEPS):
+                if step == when:
+                    quantize_wo(b, order[step])
             for last, block in last_unit.items():
                 ready = last + (1 if order[last] in folded else 3)
                 if step == ready:
                     quantize_block(*block)
-                if step == max(ready + 1, len(order) - 1 if block[1] == J else 0):
-                    output_block(*block)
+                if step == max(ready + 1, len(order) - 1 if block[1] == J else WO_STEPS[1]):
+                    (output_last_block if sum(block) == S else output_block)(*block)

@@ -19,11 +19,11 @@ ALU = mybir.AluOpType
 P = 128
 J = 128
 CENTRE, FIRST, SECOND = 0, 1, 2
-OUT_BLOCKS = ((0, 256), (256, 256), (512, 256), (768, 128), (896, 128))
+OUT_BLOCKS = ((0, 256), (256, 128), (384, 128), (512, 128), (640, 256), (896, 128))
+EARLY_ROUNDED = OUT_BLOCKS[4]
 FOLDED_FROM = 640
 HEAD = 256
-WO_STEPS = (5, 6)
-NARROW = 4
+NARROW = 6
 
 
 def tile_list_point_edge_conv_kernel(tc, tab_words, tab_scales, offs, offs2, offs3, wc, wa_words, wa_scales,
@@ -39,10 +39,10 @@ def tile_list_point_edge_conv_kernel(tc, tab_words, tab_scales, offs, offs2, off
         tab_w = shared.tile([P, T], I32, align_bytes=64, offset=49152)
         tab_s = keep.tile([P, T // 4], I32, align_bytes=64)
         wc_raw = [keep.tile([P, 4, 512], F32, name="wc_raw%d" % b) for b in range(2)]
-        wc_bf = [keep.tile([P, 2048], BF16, name="wc_bf%d" % b, align_bytes=64) for b in range(2)]
+        wc_bf = [shared.tile([P, 2048], BF16, name="wc_bf%d" % b, align_bytes=64, offset=57344 + 4096 * b) for b in range(2)]
         wc_q = keep.tile([P, H], U32, align_bytes=64)
         wc_s = keep.tile([P, H], U8, align_bytes=64)
-        wbs_raw = shared.tile([P, H // 4], I32, align_bytes=64, offset=0)
+        wbs_raw = shared.tile([P, H // 4], I32, align_bytes=64, offset=65536)
         wb_raw = keep.tile([P, H], I32, align_bytes=64)
         wa_raw = keep.tile([P, H // 2], I32, align_bytes=64)
         was_raw = shared.tile([P, H // 4], I32, align_bytes=64, offset=5120)
@@ -54,7 +54,6 @@ def tile_list_point_edge_conv_kernel(tc, tab_words, tab_scales, offs, offs2, off
         wo_bf = [shared.tile([P, 4 * N], BF16, name="wo_bf%d" % b, align_bytes=64, offset=49152 + 4096 * b) for b in range(2)]
         wo_s = keep.tile([P, 2, N], U8, align_bytes=64)
         bias = keep.tile([P, 4], F32)
-        h_bf = keep.tile([P, 2 * S * 4], BF16, align_bytes=64)
         h_q = keep.tile([P, 2 * S], U32, align_bytes=64)
         h_s = keep.tile([P, 2 * S], U8, align_bytes=64)
         res = keep.tile([P, 4, S], F32)
@@ -69,21 +68,21 @@ def tile_list_point_edge_conv_kernel(tc, tab_words, tab_scales, offs, offs2, off
                 nc.sync.dma_start(wo_raw[b][:, t, :], wo_rows[b, t])
 
         nc.gpsimd.memset(tab_s[:], 0)
-        nc.gpsimd.memset(wbs_raw[:], 0)
         nc.gpsimd.memset(was_raw[:], 0)
+        nc.gpsimd.memset(wbs_raw[:], 0)
         wc_rows = wc.rearrange("(p i) r -> p i r", i=4)
         nc.sync.dma_start(wa_raw[:], wa_words[0].bitcast(I32))
-        nc.sync.dma_start(lists[SECOND][:], offs3)
+        nc.sync.dma_start(lists[FIRST][:], offs2)
         load_scales(tab_s, tab_scales)
-        nc.sync.dma_start(wb_raw[:], wb_words[0].rearrange("p e i -> p (e i)").bitcast(I32))
         nc.sync.dma_start(tab_w[:], tab_words[0].rearrange("p t i -> p (t i)").bitcast(I32))
-        load_scales(wbs_raw, wb_scales)
+        load_scales(was_raw, wa_scales)
         nc.sync.dma_start(lists[CENTRE][:], offs)
         nc.sync.dma_start(wc_raw[0][:], wc_rows[:, :, 0:512])
         nc.sync.dma_start(wc_raw[1][:], wc_rows[:, :, 512:1024])
-        nc.sync.dma_start(lists[FIRST][:], offs2)
+        nc.sync.dma_start(wb_raw[:], wb_words[0].rearrange("p e i -> p (e i)").bitcast(I32))
+        nc.sync.dma_start(lists[SECOND][:], offs3)
+        load_scales(wbs_raw, wb_scales)
         load_wo(0)
-        load_scales(was_raw, wa_scales)
         load_wo(1)
         with nc.allow_non_contiguous_dma(reason="one bias value a partition"):
             nc.sync.dma_start(bias[:], bo.rearrange("(t p) -> p t", p=P))
@@ -132,7 +131,7 @@ def tile_list_point_edge_conv_kernel(tc, tab_words, tab_scales, offs, offs2, off
                 nc.scalar.activation(dst[:, cols], src[:, cols], ACT.Copy)
 
         def quantize_wo(b, after):
-            codes = shared.tile([P, N], U32, name="wo_q%d" % b, align_bytes=64, offset=side_offset(after))
+            codes = shared.tile([P, N], U32, name="wo_q%d" % b, align_bytes=64, offset=larger_offset(after))
             nc.vector.quantize_mx(out=codes[:].bitcast(FP8X4), scales=wo_s[:, b, :], in_=wo_bf[b][:])
             wo_q.append(codes)
 
@@ -153,11 +152,25 @@ def tile_list_point_edge_conv_kernel(tc, tab_words, tab_scales, offs, offs2, off
                                         rhs_scale=got[False, i, j0], start=(n == 0), stop=(n == len(terms) - 1))
             return bank[:].rearrange("p t j -> p j t")
 
+        h_tiles = {}
+
+        def block_of(j0):
+            return [blk for blk in OUT_BLOCKS if blk[0] <= j0 < blk[0] + blk[1]][0]
+
+        def h_tile(block):
+            if block not in h_tiles:
+                if block == EARLY_ROUNDED:
+                    tile = shared.tile([P, 8 * block[1]], BF16, name="h_bf%d" % block[0], align_bytes=64, offset=49152 + 4096)
+                else:
+                    tile = keep.tile([P, 8 * block[1]], BF16, name="h_bf%d" % block[0], align_bytes=64)
+                h_tiles.setdefault(block, tile)
+            return h_tiles[block]
+
         def h_slice(unit):
             j0, b = unit
-            first, width = [blk for blk in OUT_BLOCKS if blk[0] <= j0 < blk[0] + blk[1]][0]
-            c0 = 2 * first + b * width + j0 - first
-            return h_bf[:, 4 * c0 : 4 * (c0 + J)]
+            first, width = block_of(j0)
+            c0 = b * width + j0 - first
+            return h_tile((first, width))[:, 4 * c0 : 4 * (c0 + J)]
 
         def as_words(ap):
             return ap.rearrange("p (j t) -> p j t", t=4)
@@ -171,14 +184,17 @@ def tile_list_point_edge_conv_kernel(tc, tab_words, tab_scales, offs, offs2, off
         def side_offset(unit):
             return 8192 + 2048 * units.index(unit)
 
+        def larger_offset(unit):
+            return 66560 + 2048 * units.index(unit)
+
         def stage_side(unit):
-            bank = fill_bank((CENTRE, SECOND) if unit in folded else (SECOND,), unit)
+            bank = fill_bank((CENTRE, FIRST) if unit in folded else (FIRST,), unit)
             side = shared.tile([P, 4 * J], BF16 if unit in narrow else F32, name="side%d_%d" % unit, align_bytes=64, offset=side_offset(unit))
             nc.scalar.activation(as_words(side[:]), bank, ACT.Relu if unit in folded else ACT.Copy)
             sides.setdefault(unit, side)
 
         def stage_other(unit):
-            bank = fill_bank((CENTRE, FIRST), unit)
+            bank = fill_bank((CENTRE, SECOND), unit)
             other = keep.tile([P, 4 * J], BF16, name="other%d_%d" % unit)
             nc.scalar.activation(as_words(other[:]), bank, ACT.Copy)
             others.setdefault(unit, other)
@@ -187,11 +203,11 @@ def tile_list_point_edge_conv_kernel(tc, tab_words, tab_scales, offs, offs2, off
             if unit in narrow:
                 nc.vector.tensor_tensor(h_slice(unit), others[unit][:], sides[unit][:], ALU.max)
             elif unit in folded:
-                bank = fill_bank((CENTRE, FIRST), unit)
+                bank = fill_bank((CENTRE, SECOND), unit)
                 nc.vector.tensor_tensor(as_words(h_slice(unit)), bank, as_words(sides[unit][:]), ALU.max)
             else:
-                bank = fill_bank((FIRST,), unit)
-                larger = keep.tile([P, 4 * J], F32, name="larger%d_%d" % unit)
+                bank = fill_bank((SECOND,), unit)
+                larger = shared.tile([P, 4 * J], F32, name="larger%d_%d" % unit, align_bytes=64, offset=larger_offset(unit))
                 nc.vector.tensor_tensor(as_words(larger[:]), bank, as_words(sides[unit][:]), ALU.max)
                 largers.setdefault(unit, larger)
 
@@ -204,11 +220,11 @@ def tile_list_point_edge_conv_kernel(tc, tab_words, tab_scales, offs, offs2, off
             if unit in plain:
                 nc.scalar.activation(h_slice(unit), h_slice(unit), ACT.Relu)
 
-        def quantize_block(j0, width):
-            step = J if j0 + width == S else 2 * width
-            for c0 in range(2 * j0, 2 * (j0 + width), step):
-                nc.vector.quantize_mx(out=h_q[:, c0 : c0 + step].bitcast(FP8X4), scales=h_s[:, c0 : c0 + step],
-                                      in_=h_bf[:, 4 * c0 : 4 * (c0 + step)])
+        def quantize_h(block, first_half=0, halves=2):
+            j0, width = block
+            lo, hi = first_half * width, (first_half + halves) * width
+            nc.vector.quantize_mx(out=h_q[:, 2 * j0 + lo : 2 * j0 + hi].bitcast(FP8X4), scales=h_s[:, 2 * j0 + lo : 2 * j0 + hi],
+                                  in_=h_tile(block)[:, 4 * lo : 4 * hi])
 
         out_rows = out.rearrange("(t p) j -> p t j", p=P)
 
@@ -229,6 +245,26 @@ def tile_list_point_edge_conv_kernel(tc, tab_words, tab_scales, offs, offs2, off
                     nc.scalar.activation(res[:, nt, cols], bank[:, e, 0:width], ACT.Relu, bias=bias[:, nt : nt + 1])
                 nc.sync.dma_start(out_rows[:, 2 * pair : 2 * pair + 2, cols], res[:, 2 * pair : 2 * pair + 2, cols])
 
+        def output_narrow(j0, width):
+            cols = slice(j0, j0 + width)
+            bank = psum2.tile([P, 4, J], F32, name="bank")
+            for nt in range(4):
+                for b in range(2):
+                    second_layer(bank[:, nt, :], nt, b, j0, width)
+            for nt in range(4):
+                nc.scalar.activation(res[:, nt, cols], bank[:, nt, :], ACT.Relu, bias=bias[:, nt : nt + 1])
+            nc.sync.dma_start(out_rows[:, :, cols], res[:, :, cols])
+
+        def output_on_vector(j0, width):
+            cols = slice(j0, j0 + width)
+            bank = psum1.tile([P, 4, J], F32, name="bank")
+            for nt in range(4):
+                for b in range(2):
+                    second_layer(bank[:, nt, :], nt, b, j0, width)
+            for nt in range(4):
+                nc.vector.tensor_scalar(res[:, nt, cols], bank[:, nt, :], bias[:, nt : nt + 1], 0.0, ALU.add, ALU.max)
+            nc.sync.dma_start(out_rows[:, :, cols], res[:, :, cols])
+
         def output_last_block(j0, width):
             cols = slice(j0, j0 + width)
             banks = [psum1.tile([P, 2, 256], F32, name="bank") for nt in range(2)] + [psum2.tile([P, 2, 256], F32, name="bank") for nt in range(2)]
@@ -243,41 +279,62 @@ def tile_list_point_edge_conv_kernel(tc, tab_words, tab_scales, offs, offs2, off
                     nc.sync.dma_start(out_rows[:, nt - 1 : nt + 1, cols], res[:, nt - 1 : nt + 1, cols])
 
         deal_columns(wa_q, wa_raw, 2)
-        gather_scales(SECOND)
-        deal_columns(wb_q, wb_raw, 4)
-        gather(tab_w, U32, SECOND, 0, HEAD, keep.tile([P, HEAD], U32, name="got_w2_head", align_bytes=64))
-        deal_scales(wb_s, wbs_raw)
-        gather(tab_w, U32, SECOND, HEAD, S - HEAD, shared.tile([P, S - HEAD], U32, name="got_w2_rest", align_bytes=64, offset=0))
-        gather_scales(CENTRE)
-        gather_words(CENTRE)
-        quantize_wc(0)
-        quantize_wc(1)
         gather_scales(FIRST)
         gather(tab_w, U32, FIRST, 0, HEAD, keep.tile([P, HEAD], U32, name="got_w1_head", align_bytes=64))
         deal_scales(wa_s, was_raw)
         gather(tab_w, U32, FIRST, HEAD, S - HEAD, shared.tile([P, S - HEAD], U32, name="got_w1_rest", align_bytes=64, offset=5120))
-        for unit in plain + [u for u in folded if u[1] == 0]:
+        gather_scales(CENTRE)
+        gather_words(CENTRE)
+        quantize_wc(0)
+        gather(tab_s, U8, SECOND, 0, S, shared.tile([P, S], U8, name="got_s2", align_bytes=64, offset=57344))
+        quantize_wc(1)
+        deal_columns(wb_q, wb_raw, 4)
+        deal_scales(wb_s, wbs_raw)
+        gather(tab_w, U32, SECOND, 0, HEAD, shared.tile([P, HEAD], U32, name="got_w2_head", align_bytes=64, offset=61440))
+        gather(tab_w, U32, SECOND, HEAD, S - HEAD, shared.tile([P, S - HEAD], U32, name="got_w2_rest", align_bytes=64, offset=63488))
+        for unit in plain + [u for u in folded if u[1] == 0] + [u for u in folded if u[1] == 1]:
             stage_side(unit)
-        late_sides = [u for u in folded if u[1] == 1]
         cast_wo_on_gpsimd(0)
         cast_wo_on_gpsimd(1)
 
-        order = plain + folded
-        last_unit = {max(n for n, u in enumerate(order) if j0 <= u[0] < j0 + width): (j0, width) for j0, width in OUT_BLOCKS}
-        for step in range(len(order) + 6):
-            for lag, stage in enumerate((stage_max, stage_diff, stage_relu)):
-                if 0 <= step - lag < len(order):
-                    stage(order[step - lag])
-            if 1 <= step <= len(late_sides):
-                stage_side(late_sides[step - 1])
-            if 0 <= step - 4 < len(narrow):
-                stage_other(narrow[step - 4])
-            for b, when in enumerate(WO_STEPS):
-                if step == when:
-                    quantize_wo(b, order[step])
-            for last, block in last_unit.items():
-                ready = last + (1 if order[last] in folded else 3)
-                if step == ready:
-                    quantize_block(*block)
-                if step == max(ready + 1, len(order) - 1 if block[1] == J else WO_STEPS[1]):
-                    (output_last_block if sum(block) == S else output_block)(*block)
+        def plain_step(n):
+            if n < len(plain):
+                stage_max(plain[n])
+            if 1 <= n <= len(plain):
+                stage_diff(plain[n - 1])
+            if 2 <= n:
+                stage_relu(plain[n - 2])
+
+        for n in range(6):
+            plain_step(n)
+            if 1 <= n <= 4:
+                stage_other(narrow[n - 1])
+        stage_other(narrow[4])
+        stage_other(narrow[5])
+        quantize_wo(0, plain[4])
+        quantize_wo(1, plain[3])
+        quantize_h(OUT_BLOCKS[0])
+        stage_max(narrow[0])
+        stage_max(narrow[1])
+        stage_max(narrow[2])
+        stage_max(narrow[3])
+        stage_max(narrow[4])
+        stage_max(narrow[5])
+        quantize_h(OUT_BLOCKS[4])
+        output_block(*OUT_BLOCKS[0])
+        plain_step(6)
+        quantize_h(OUT_BLOCKS[5])
+        output_block(*OUT_BLOCKS[4])
+        plain_step(7)
+        quantize_h(OUT_BLOCKS[1])
+        output_narrow(*OUT_BLOCKS[5])
+        plain_step(8)
+        output_narrow(*OUT_BLOCKS[1])
+        plain_step(9)
+        quantize_h(OUT_BLOCKS[2])
+        plain_step(10)
+        plain_step(11)
+        quantize_h(OUT_BLOCKS[3], 0, 1)
+        output_on_vector(*OUT_BLOCKS[2])
+        quantize_h(OUT_BLOCKS[3], 1, 1)
+        output_last_block(*OUT_BLOCKS[3])

@@ -1,6 +1,7 @@
 from contextlib import ExitStack
 
 import concourse.mybir as mybir
+from concourse.masks import make_identity
 
 K, T, S, H, N = 512, 2048, 1024, 1024, 512
 FLOPS = 2 * (3 * K * H * S + H * N * S)
@@ -24,6 +25,9 @@ EARLY_ROUNDED = OUT_BLOCKS[4]
 FOLDED_FROM = 640
 HEAD = 256
 NARROW = 6
+TURNED = (4, 6)
+ON_GPSIMD = (6, 7)
+F32_MAX = 3.4028234663852886e38
 
 
 def tile_list_point_edge_conv_kernel(tc, tab_words, tab_scales, offs, offs2, offs3, wc, wa_words, wa_scales,
@@ -51,10 +55,9 @@ def tile_list_point_edge_conv_kernel(tc, tab_words, tab_scales, offs, offs2, off
         wa_s = keep.tile([P, H // 4], I32, align_bytes=64)
         wb_s = keep.tile([P, H // 4], I32, align_bytes=64)
         wo_raw = [keep.tile([P, 4, N], F32, name="wo_raw%d" % b) for b in range(2)]
-        wo_bf = [shared.tile([P, 4 * N], BF16, name="wo_bf%d" % b, align_bytes=64, offset=49152 + 4096 * b) for b in range(2)]
+        wo_bf = shared.tile([P, 2, 4 * N], BF16, align_bytes=64, offset=49152)
         wo_s = keep.tile([P, 2, N], U8, align_bytes=64)
         bias = keep.tile([P, 4], F32)
-        h_q = keep.tile([P, 2 * S], U32, align_bytes=64)
         h_s = keep.tile([P, 2 * S], U8, align_bytes=64)
         res = keep.tile([P, 4, S], F32)
 
@@ -70,6 +73,8 @@ def tile_list_point_edge_conv_kernel(tc, tab_words, tab_scales, offs, offs2, off
         nc.gpsimd.memset(tab_s[:], 0)
         nc.gpsimd.memset(was_raw[:], 0)
         nc.gpsimd.memset(wbs_raw[:], 0)
+        identity = keep.tile([P, P], F32)
+        make_identity(nc, identity[:])
         wc_rows = wc.rearrange("(p i) r -> p i r", i=4)
         nc.sync.dma_start(wa_raw[:], wa_words[0].bitcast(I32))
         nc.sync.dma_start(lists[FIRST][:], offs2)
@@ -105,8 +110,8 @@ def tile_list_point_edge_conv_kernel(tc, tab_words, tab_scales, offs, offs2, off
                                   src[:].rearrange("p (b u t s) -> p b t u s", b=2, t=4, s=run))
 
         def deal_scales(dst, src):
-            nc.vector.tensor_copy(dst[:].rearrange("p (b t u) -> p b t u", b=2, t=4),
-                                  src[:].rearrange("p (b u t) -> p b t u", b=2, t=4))
+            nc.vector.tensor_copy(dst[:].rearrange("p (b t g u) -> p b g t u", b=2, t=4, u=4),
+                                  src[:].rearrange("p (b g u t) -> p b g t u", b=2, t=4, u=4))
 
         def quantize_wc(b):
             src = wc_raw[b][:].rearrange("p i (u t s) -> p t u i s", t=4, s=4)
@@ -120,27 +125,21 @@ def tile_list_point_edge_conv_kernel(tc, tab_words, tab_scales, offs, offs2, off
 
         def cast_wo_on_gpsimd(b):
             src = wo_raw[b][:].rearrange("p t n -> p n t")
-            dst = wo_bf[b][:].rearrange("p (n t) -> p n t", t=4)
+            dst = wo_bf[:, b, :].rearrange("p (n t) -> p n t", t=4)
             nc.gpsimd.tensor_scalar(dst, src, 1.0, 0.0, ALU.mult, ALU.add)
 
-        def cast_wo_on_scalar(b):
-            src = wo_raw[b][:].rearrange("p t (c s) -> p c t s", s=4)
-            dst = wo_bf[b][:].rearrange("p (c s t) -> p c t s", s=4, t=4)
-            for half in range(2):
-                cols = slice(64 * half, 64 * (half + 1))
-                nc.scalar.activation(dst[:, cols], src[:, cols], ACT.Copy)
-
-        def quantize_wo(b, after):
-            codes = shared.tile([P, N], U32, name="wo_q%d" % b, align_bytes=64, offset=larger_offset(after))
-            nc.vector.quantize_mx(out=codes[:].bitcast(FP8X4), scales=wo_s[:, b, :], in_=wo_bf[b][:])
+        def quantize_wo(after):
+            codes = shared.tile([P, 2, N], U32, name="wo_q", align_bytes=64, offset=side_offset(after))
+            nc.vector.quantize_mx(out=codes[:].rearrange("p b n -> p (b n)").bitcast(FP8X4), scales=wo_s[:].rearrange("p b n -> p (b n)"),
+                                  in_=wo_bf[:].rearrange("p b n -> p (b n)"))
             wo_q.append(codes)
 
-        def weights(i, col):
+        def weights(i, col, n=P):
             if i == CENTRE:
-                return wc_q[:, col : col + P].bitcast(FP8X4), wc_s[:, col : col + P]
+                return wc_q[:, col : col + n].bitcast(FP8X4), wc_s[:, col : col + n]
             if i == FIRST:
-                return wa_q[:].bitcast(U8)[:, 2 * col : 2 * (col + P)].bitcast(FP4X4), wa_s[:].bitcast(U8)[:, col : col + P]
-            return wb_q[:, col : col + P].bitcast(FP8X4), wb_s[:].bitcast(U8)[:, col : col + P]
+                return wa_q[:].bitcast(U8)[:, 2 * col : 2 * (col + n)].bitcast(FP4X4), wa_s[:].bitcast(U8)[:, col : col + n]
+            return wb_q[:, col : col + n].bitcast(FP8X4), wb_s[:].bitcast(U8)[:, col : col + n]
 
         def fill_bank(terms, unit):
             j0, b = unit
@@ -152,15 +151,26 @@ def tile_list_point_edge_conv_kernel(tc, tab_words, tab_scales, offs, offs2, off
                                         rhs_scale=got[False, i, j0], start=(n == 0), stop=(n == len(terms) - 1))
             return bank[:].rearrange("p t j -> p j t")
 
-        h_tiles = {}
+        def fill_turned(i, unit):
+            j0, b = unit
+            bank = psum1.tile([P, 4 * P], F32, name="bank")
+            w_codes, w_scales = weights(i, 512 * b, 512)
+            nc.tensor.matmul_mx(out=bank[:], lhsT=got[True, i, j0].bitcast(FP8X4), lhsT_scale=got[False, i, j0],
+                                rhs=w_codes, rhs_scale=w_scales, start=True, stop=True)
+            return bank[:]
+
+        h_tiles, h_q = {}, {}
 
         def block_of(j0):
             return [blk for blk in OUT_BLOCKS if blk[0] <= j0 < blk[0] + blk[1]][0]
 
         def h_tile(block):
             if block not in h_tiles:
-                if block == EARLY_ROUNDED:
-                    tile = shared.tile([P, 8 * block[1]], BF16, name="h_bf%d" % block[0], align_bytes=64, offset=49152 + 4096)
+                if block[0] >= FOLDED_FROM:
+                    tile = shared.tile([P, 8 * block[1]], BF16, name="h_bf%d" % block[0], align_bytes=64,
+                                       offset=49152 + (4096 if block == EARLY_ROUNDED else 2048))
+                elif block == OUT_BLOCKS[2]:
+                    tile = shared.tile([P, 8 * block[1]], BF16, name="h_bf%d" % block[0], align_bytes=64, offset=0)
                 else:
                     tile = keep.tile([P, 8 * block[1]], BF16, name="h_bf%d" % block[0], align_bytes=64)
                 h_tiles.setdefault(block, tile)
@@ -172,6 +182,16 @@ def tile_list_point_edge_conv_kernel(tc, tab_words, tab_scales, offs, offs2, off
             c0 = b * width + j0 - first
             return h_tile((first, width))[:, 4 * c0 : 4 * (c0 + J)]
 
+        def block_slice(tiles, name, unit):
+            j0, b = unit
+            block = block_of(j0)
+            if block not in tiles and name == "other" and block == OUT_BLOCKS[5]:
+                tiles.setdefault(block, shared.tile([P, 8 * block[1]], BF16, name="other_late", align_bytes=64, offset=0))
+            if block not in tiles:
+                tiles.setdefault(block, keep.tile([P, 8 * block[1]], BF16, name="%s_bf%d" % (name, block[0]), align_bytes=64))
+            c0 = b * block[1] + j0 - block[0]
+            return tiles[block][:, 4 * c0 : 4 * (c0 + J)]
+
         def as_words(ap):
             return ap.rearrange("p (j t) -> p j t", t=4)
 
@@ -179,29 +199,55 @@ def tile_list_point_edge_conv_kernel(tc, tab_words, tab_scales, offs, offs2, off
         plain = [u for u in units if u[0] < FOLDED_FROM]
         folded = [u for u in units if u[0] >= FOLDED_FROM]
         narrow = folded[:NARROW]
-        sides, largers, others = {}, {}, {}
+        sides, largers, others, rounded_sides = {}, {}, {}, {}
 
         def side_offset(unit):
-            return 8192 + 2048 * units.index(unit)
+            return 8192 + 3072 * units.index(unit)
 
         def larger_offset(unit):
             return 66560 + 2048 * units.index(unit)
 
+        turned = plain[TURNED[0] : TURNED[1]]
+        centres = {}
+
+        def stage_centre(unit):
+            centre = keep.tile([P, 4 * P], F32, name="centre%d_%d" % unit)
+            nc.scalar.activation(centre[:], fill_turned(CENTRE, unit), ACT.Copy)
+            centres.setdefault(unit, centre)
+
+        def stage_turn(unit):
+            bank = psum2.tile([P, 4, J], F32, name="bank")
+            for t in range(4):
+                for n, term in enumerate((largers[unit], centres[unit])):
+                    nc.tensor.matmul(bank[:, t, :], term[:, P * t : P * (t + 1)], identity[:], start=(n == 0), stop=(n == 1), is_transpose=True)
+            nc.scalar.activation(as_words(h_slice(unit)), bank[:].rearrange("p t j -> p j t"), ACT.Relu)
+
         def stage_side(unit):
+            if unit in turned:
+                side = shared.tile([P, 4 * J], F32, name="side%d_%d" % unit, align_bytes=64, offset=side_offset(unit))
+                nc.scalar.activation(side[:], fill_turned(FIRST, unit), ACT.Copy)
+                sides.setdefault(unit, side)
+                return
             bank = fill_bank((CENTRE, FIRST) if unit in folded else (FIRST,), unit)
-            side = shared.tile([P, 4 * J], BF16 if unit in narrow else F32, name="side%d_%d" % unit, align_bytes=64, offset=side_offset(unit))
+            if unit in narrow:
+                nc.scalar.activation(as_words(block_slice(rounded_sides, "side", unit)), bank, ACT.Relu)
+                return
+            side = shared.tile([P, 4 * J], F32, name="side%d_%d" % unit, align_bytes=64, offset=side_offset(unit))
             nc.scalar.activation(as_words(side[:]), bank, ACT.Relu if unit in folded else ACT.Copy)
             sides.setdefault(unit, side)
 
         def stage_other(unit):
-            bank = fill_bank((CENTRE, SECOND), unit)
-            other = keep.tile([P, 4 * J], BF16, name="other%d_%d" % unit)
-            nc.scalar.activation(as_words(other[:]), bank, ACT.Copy)
-            others.setdefault(unit, other)
+            bank = fill_bank((SECOND, CENTRE), unit)
+            nc.scalar.activation(as_words(block_slice(others, "other", unit)), bank, ACT.Copy)
+
+        def rounded_max(block):
+            nc.vector.tensor_tensor(h_tile(block)[:], others[block][:], rounded_sides[block][:], ALU.max)
 
         def stage_max(unit):
-            if unit in narrow:
-                nc.vector.tensor_tensor(h_slice(unit), others[unit][:], sides[unit][:], ALU.max)
+            if unit in turned:
+                larger = shared.tile([P, 4 * J], F32, name="larger%d_%d" % unit, align_bytes=64, offset=larger_offset(unit))
+                nc.vector.tensor_tensor(larger[:], fill_turned(SECOND, unit), sides[unit][:], ALU.max)
+                largers.setdefault(unit, larger)
             elif unit in folded:
                 bank = fill_bank((CENTRE, SECOND), unit)
                 nc.vector.tensor_tensor(as_words(h_slice(unit)), bank, as_words(sides[unit][:]), ALU.max)
@@ -217,21 +263,28 @@ def tile_list_point_edge_conv_kernel(tc, tab_words, tab_scales, offs, offs2, off
                 nc.vector.tensor_tensor(as_words(h_slice(unit)), bank, as_words(largers[unit][:]), ALU.add)
 
         def stage_relu(unit):
-            if unit in plain:
+            if plain.index(unit) in ON_GPSIMD:
+                nc.gpsimd.tensor_scalar(h_slice(unit), h_slice(unit), F32_MAX, 0.0, ALU.min, ALU.max)
+            else:
                 nc.scalar.activation(h_slice(unit), h_slice(unit), ACT.Relu)
 
         def quantize_h(block, first_half=0, halves=2):
             j0, width = block
             lo, hi = first_half * width, (first_half + halves) * width
-            nc.vector.quantize_mx(out=h_q[:, 2 * j0 + lo : 2 * j0 + hi].bitcast(FP8X4), scales=h_s[:, 2 * j0 + lo : 2 * j0 + hi],
+            if block not in h_q:
+                if j0 == 0:
+                    h_q.setdefault(block, shared.tile([P, 2 * width], U32, name="h_q0", align_bytes=64, offset=side_offset(plain[6]) + 1024))
+                else:
+                    h_q.setdefault(block, keep.tile([P, 2 * width], U32, name="h_q%d" % j0, align_bytes=64))
+            nc.vector.quantize_mx(out=h_q[block][:, lo:hi].bitcast(FP8X4), scales=h_s[:, 2 * j0 + lo : 2 * j0 + hi],
                                   in_=h_tile(block)[:, 4 * lo : 4 * hi])
 
         out_rows = out.rearrange("(t p) j -> p t j", p=P)
 
         def second_layer(dst, nt, b, j0, width):
             h_cols = slice(2 * j0 + b * width, 2 * j0 + (b + 1) * width)
-            nc.tensor.matmul_mx(out=dst, lhsT=wo_q[b][:, P * nt : P * (nt + 1)].bitcast(FP8X4), lhsT_scale=wo_s[:, b, P * nt : P * (nt + 1)],
-                                rhs=h_q[:, h_cols].bitcast(FP8X4), rhs_scale=h_s[:, h_cols], start=(b == 0), stop=(b == 1))
+            nc.tensor.matmul_mx(out=dst, lhsT=wo_q[0][:, b, P * nt : P * (nt + 1)].bitcast(FP8X4), lhsT_scale=wo_s[:, b, P * nt : P * (nt + 1)],
+                                rhs=h_q[j0, width][:, b * width : (b + 1) * width].bitcast(FP8X4), rhs_scale=h_s[:, h_cols], start=(b == 0), stop=(b == 1))
 
         def output_block(j0, width):
             cols = slice(j0, j0 + width)
@@ -255,19 +308,24 @@ def tile_list_point_edge_conv_kernel(tc, tab_words, tab_scales, offs, offs2, off
                 nc.scalar.activation(res[:, nt, cols], bank[:, nt, :], ACT.Relu, bias=bias[:, nt : nt + 1])
             nc.sync.dma_start(out_rows[:, :, cols], res[:, :, cols])
 
-        def output_on_vector(j0, width):
+        def output_shared(j0, width):
             cols = slice(j0, j0 + width)
-            bank = psum1.tile([P, 4, J], F32, name="bank")
-            for nt in range(4):
-                for b in range(2):
-                    second_layer(bank[:, nt, :], nt, b, j0, width)
-            for nt in range(4):
-                nc.vector.tensor_scalar(res[:, nt, cols], bank[:, nt, :], bias[:, nt : nt + 1], 0.0, ALU.add, ALU.max)
+            for pair in range(2):
+                bank = psum2.tile([P, 2, J], F32, name="bank")
+                for e in range(2):
+                    for b in range(2):
+                        second_layer(bank[:, e, :], 2 * pair + e, b, j0, width)
+                for e in range(2):
+                    nt = 2 * pair + e
+                    if pair == 0:
+                        nc.vector.tensor_scalar(res[:, nt, cols], bank[:, e, :], bias[:, nt : nt + 1], 0.0, ALU.add, ALU.max)
+                    else:
+                        nc.scalar.activation(res[:, nt, cols], bank[:, e, :], ACT.Relu, bias=bias[:, nt : nt + 1])
             nc.sync.dma_start(out_rows[:, :, cols], res[:, :, cols])
 
         def output_last_block(j0, width):
             cols = slice(j0, j0 + width)
-            banks = [psum1.tile([P, 2, 256], F32, name="bank") for nt in range(2)] + [psum2.tile([P, 2, 256], F32, name="bank") for nt in range(2)]
+            banks = [psum1.tile([P, 2, 256], F32, name="bank") for nt in range(4)]
             for b in range(2):
                 for nt in range(4):
                     second_layer(banks[nt][:, 0, 0:width], nt, b, j0, width)
@@ -302,39 +360,45 @@ def tile_list_point_edge_conv_kernel(tc, tab_words, tab_scales, offs, offs2, off
                 stage_max(plain[n])
             if 1 <= n <= len(plain):
                 stage_diff(plain[n - 1])
-            if 2 <= n:
+            if 2 <= n and plain[n - 2] not in turned:
                 stage_relu(plain[n - 2])
 
-        for n in range(6):
+        reads = [(stage_other, u) for u in folded]
+        B0, C1, C2, C3, EARLY, LATE = OUT_BLOCKS
+        for n in range(5):
             plain_step(n)
-            if 1 <= n <= 4:
-                stage_other(narrow[n - 1])
-        stage_other(narrow[4])
-        stage_other(narrow[5])
-        quantize_wo(0, plain[4])
-        quantize_wo(1, plain[3])
-        quantize_h(OUT_BLOCKS[0])
-        stage_max(narrow[0])
-        stage_max(narrow[1])
-        stage_max(narrow[2])
-        stage_max(narrow[3])
-        stage_max(narrow[4])
-        stage_max(narrow[5])
-        quantize_h(OUT_BLOCKS[4])
-        output_block(*OUT_BLOCKS[0])
-        plain_step(6)
-        quantize_h(OUT_BLOCKS[5])
-        output_block(*OUT_BLOCKS[4])
+            if n >= 1:
+                stage, unit = reads[n - 1]
+                stage(unit)
+        stage_max(plain[5])
+        stage_relu(plain[3])
+        stage, unit = reads[4]
+        stage(unit)
+        stage_max(plain[6])
+        for stage, unit in reads[5:]:
+            stage(unit)
+        for unit in turned:
+            stage_centre(unit)
+        for unit in turned:
+            stage_turn(unit)
+        quantize_wo(plain[5])
+        quantize_h(B0)
+        rounded_max(EARLY)
+        rounded_max(LATE)
+        quantize_h(EARLY)
+        quantize_h(LATE)
+        quantize_h(C1)
+        output_block(*B0)
+        output_block(*EARLY)
         plain_step(7)
-        quantize_h(OUT_BLOCKS[1])
-        output_narrow(*OUT_BLOCKS[5])
         plain_step(8)
-        output_narrow(*OUT_BLOCKS[1])
+        output_narrow(*LATE)
         plain_step(9)
-        quantize_h(OUT_BLOCKS[2])
+        output_narrow(*C1)
+        quantize_h(C2)
         plain_step(10)
         plain_step(11)
-        quantize_h(OUT_BLOCKS[3], 0, 1)
-        output_on_vector(*OUT_BLOCKS[2])
-        quantize_h(OUT_BLOCKS[3], 1, 1)
-        output_last_block(*OUT_BLOCKS[3])
+        quantize_h(C3, 0, 1)
+        output_shared(*C2)
+        quantize_h(C3, 1, 1)
+        output_last_block(*C3)

@@ -321,7 +321,7 @@ def tile_list_point_edge_conv_kernel(tc, tab_words, tab_scales, offs, offs2, off
                         nc.vector.tensor_scalar(res[:, nt, cols], bank[:, e, :], bias[:, nt : nt + 1], 0.0, ALU.add, ALU.max)
                     else:
                         nc.scalar.activation(res[:, nt, cols], bank[:, e, :], ACT.Relu, bias=bias[:, nt : nt + 1])
-            nc.sync.dma_start(out_rows[:, :, cols], res[:, :, cols])
+                nc.sync.dma_start(out_rows[:, 2 * pair : 2 * pair + 2, cols], res[:, 2 * pair : 2 * pair + 2, cols])
 
         def output_last_block(j0, width):
             cols = slice(j0, j0 + width)

@@ -19,15 +19,13 @@ ALU = mybir.AluOpType
 
 P = 128
 J = 128
+KB = 1024
 CENTRE, FIRST, SECOND = 0, 1, 2
-OUT_BLOCKS = ((0, 256), (256, 128), (384, 128), (512, 128), (640, 256), (896, 128))
-EARLY_ROUNDED = OUT_BLOCKS[4]
-FOLDED_FROM = 640
-HEAD = 256
-NARROW = 6
-TURNED = (4, 6)
-ON_GPSIMD = (6, 7)
 F32_MAX = 3.4028234663852886e38
+
+FOLD = 768
+WIDE = ((0, 256), (256, 256), (512, 256))
+LAST = ((768, 128), (896, 128))
 
 
 def tile_list_point_edge_conv_kernel(tc, tab_words, tab_scales, offs, offs2, offs3, wc, wa_words, wa_scales,
@@ -36,29 +34,32 @@ def tile_list_point_edge_conv_kernel(tc, tab_words, tab_scales, offs, offs2, off
     with ExitStack() as ctx:
         keep = ctx.enter_context(tc.tile_pool(name="keep", bufs=1))
         shared = ctx.enter_context(tc.tile_pool(name="shared", bufs=1))
-        psum1 = ctx.enter_context(tc.psum_pool(name="psum1", bufs=6))
-        psum2 = ctx.enter_context(tc.psum_pool(name="psum2", bufs=2))
+        psum = ctx.enter_context(tc.psum_pool(name="psum", bufs=1))
+
+        def at(kb, shape, dtype, name):
+            return shared.tile(shape, dtype, name=name, align_bytes=64, offset=int(kb * KB))
+
+        fills = []
+
+        def next_bank(shape):
+            fills.append(len(fills))
+            return psum.tile(shape, F32, name="bank%d" % fills[-1], offset=2048 * (fills[-1] % 8))
 
         lists = [keep.tile([P, S // 16], U16, name="list%d" % i) for i in range(3)]
-        tab_w = shared.tile([P, T], I32, align_bytes=64, offset=49152)
+        tab_w = at(0, [P, T], I32, "tab_w")
         tab_s = keep.tile([P, T // 4], I32, align_bytes=64)
-        wc_raw = [keep.tile([P, 4, 512], F32, name="wc_raw%d" % b) for b in range(2)]
-        wc_bf = [shared.tile([P, 2048], BF16, name="wc_bf%d" % b, align_bytes=64, offset=57344 + 4096 * b) for b in range(2)]
+        wc_raw = [at((12, 36)[b], [P, 4, 512], F32, "wc_raw%d" % b) for b in range(2)]
+        wc_bf = [at((20, 8)[b], [P, 2048], BF16, "wc_bf%d" % b) for b in range(2)]
         wc_q = keep.tile([P, H], U32, align_bytes=64)
         wc_s = keep.tile([P, H], U8, align_bytes=64)
-        wbs_raw = shared.tile([P, H // 4], I32, align_bytes=64, offset=65536)
-        wb_raw = keep.tile([P, H], I32, align_bytes=64)
+        wb_raw = at(26, [P, H], I32, "wb_raw")
+        wbs_raw = at(31, [P, H // 4], I32, "wbs_raw")
         wa_raw = keep.tile([P, H // 2], I32, align_bytes=64)
-        was_raw = shared.tile([P, H // 4], I32, align_bytes=64, offset=5120)
+        was_raw = keep.tile([P, H // 4], I32, align_bytes=64)
         wa_q = keep.tile([P, H // 2], I32, align_bytes=64)
-        wb_q = keep.tile([P, H], I32, align_bytes=64)
-        wa_s = keep.tile([P, H // 4], I32, align_bytes=64)
-        wb_s = keep.tile([P, H // 4], I32, align_bytes=64)
         wo_raw = [keep.tile([P, 4, N], F32, name="wo_raw%d" % b) for b in range(2)]
-        wo_bf = shared.tile([P, 2, 4 * N], BF16, align_bytes=64, offset=49152)
         wo_s = keep.tile([P, 2, N], U8, align_bytes=64)
         bias = keep.tile([P, 4], F32)
-        h_s = keep.tile([P, 2 * S], U8, align_bytes=64)
         res = keep.tile([P, 4, S], F32)
 
         def load_scales(dst, src):
@@ -79,14 +80,14 @@ def tile_list_point_edge_conv_kernel(tc, tab_words, tab_scales, offs, offs2, off
         nc.sync.dma_start(wa_raw[:], wa_words[0].bitcast(I32))
         nc.sync.dma_start(lists[FIRST][:], offs2)
         load_scales(tab_s, tab_scales)
-        nc.sync.dma_start(tab_w[:], tab_words[0].rearrange("p t i -> p (t i)").bitcast(I32))
-        load_scales(was_raw, wa_scales)
         nc.sync.dma_start(lists[CENTRE][:], offs)
         nc.sync.dma_start(wc_raw[0][:], wc_rows[:, :, 0:512])
-        nc.sync.dma_start(wc_raw[1][:], wc_rows[:, :, 512:1024])
+        nc.sync.dma_start(tab_w[:], tab_words[0].rearrange("p t i -> p (t i)").bitcast(I32))
+        load_scales(was_raw, wa_scales)
         nc.sync.dma_start(wb_raw[:], wb_words[0].rearrange("p e i -> p (e i)").bitcast(I32))
         nc.sync.dma_start(lists[SECOND][:], offs3)
         load_scales(wbs_raw, wb_scales)
+        nc.sync.dma_start(wc_raw[1][:], wc_rows[:, :, 512:1024])
         load_wo(0)
         load_wo(1)
         with nc.allow_non_contiguous_dma(reason="one bias value a partition"):
@@ -99,40 +100,25 @@ def tile_list_point_edge_conv_kernel(tc, tab_words, tab_scales, offs, offs2, off
             for j0 in range(first, first + count, J):
                 got.setdefault((dtype == U32, i, j0), dst[:, j0 - first : j0 - first + J])
 
-        def gather_scales(i):
-            gather(tab_s, U8, i, 0, S, keep.tile([P, S], U8, name="got_s%d" % i, align_bytes=64))
+        def vector_move(dst, src):
+            nc.vector.tensor_copy(dst.bitcast(I32), src.bitcast(I32))
 
-        def gather_words(i):
-            gather(tab_w, U32, i, 0, S, keep.tile([P, S], U32, name="got_w%d" % i, align_bytes=64))
+        def deal_columns(move, dst, src, run):
+            move(dst[:].bitcast(U32).rearrange("p (b t u s) -> p b t u s", b=2, t=4, s=run),
+                 src[:].bitcast(U32).rearrange("p (b u t s) -> p b t u s", b=2, t=4, s=run))
 
-        def deal_columns(dst, src, run):
-            nc.vector.tensor_copy(dst[:].rearrange("p (b t u s) -> p b t u s", b=2, t=4, s=run),
-                                  src[:].rearrange("p (b u t s) -> p b t u s", b=2, t=4, s=run))
+        def deal_scales(move, dst, src):
+            move(dst[:].bitcast(U32).rearrange("p (b t g u) -> p b g t u", b=2, t=4, u=4),
+                 src[:].bitcast(U32).rearrange("p (b g u t) -> p b g t u", b=2, t=4, u=4))
 
-        def deal_scales(dst, src):
-            nc.vector.tensor_copy(dst[:].rearrange("p (b t g u) -> p b g t u", b=2, t=4, u=4),
-                                  src[:].rearrange("p (b g u t) -> p b g t u", b=2, t=4, u=4))
-
-        def quantize_wc(b):
+        def cast_wc(b):
             src = wc_raw[b][:].rearrange("p i (u t s) -> p t u i s", t=4, s=4)
             dst = wc_bf[b][:].rearrange("p (t u s i) -> p t u i s", t=4, s=4, i=4)
             for t in range(4):
                 nc.scalar.activation(dst[:, t], src[:, t], ACT.Copy, scale=-1.0)
-            nc.vector.quantize_mx(out=wc_q[:, 512 * b : 512 * (b + 1)].bitcast(FP8X4), scales=wc_s[:, 512 * b : 512 * (b + 1)],
-                                  in_=wc_bf[b][:])
 
-        wo_q = []
-
-        def cast_wo_on_gpsimd(b):
-            src = wo_raw[b][:].rearrange("p t n -> p n t")
-            dst = wo_bf[:, b, :].rearrange("p (n t) -> p n t", t=4)
-            nc.gpsimd.tensor_scalar(dst, src, 1.0, 0.0, ALU.mult, ALU.add)
-
-        def quantize_wo(after):
-            codes = shared.tile([P, 2, N], U32, name="wo_q", align_bytes=64, offset=side_offset(after))
-            nc.vector.quantize_mx(out=codes[:].rearrange("p b n -> p (b n)").bitcast(FP8X4), scales=wo_s[:].rearrange("p b n -> p (b n)"),
-                                  in_=wo_bf[:].rearrange("p b n -> p (b n)"))
-            wo_q.append(codes)
+        def quantize_wc(b):
+            nc.vector.quantize_mx(out=wc_q[:, 512 * b : 512 * (b + 1)].bitcast(FP8X4), scales=wc_s[:, 512 * b : 512 * (b + 1)], in_=wc_bf[b][:])
 
         def weights(i, col, n=P):
             if i == CENTRE:
@@ -143,7 +129,7 @@ def tile_list_point_edge_conv_kernel(tc, tab_words, tab_scales, offs, offs2, off
 
         def fill_bank(terms, unit):
             j0, b = unit
-            bank = psum1.tile([P, 4, J], F32, name="bank")
+            bank = next_bank([P, 4, J])
             for t in range(4):
                 for n, i in enumerate(terms):
                     w_codes, w_scales = weights(i, 512 * b + P * t)
@@ -153,252 +139,225 @@ def tile_list_point_edge_conv_kernel(tc, tab_words, tab_scales, offs, offs2, off
 
         def fill_turned(i, unit):
             j0, b = unit
-            bank = psum1.tile([P, 4 * P], F32, name="bank")
+            bank = next_bank([P, 4 * P])
             w_codes, w_scales = weights(i, 512 * b, 512)
             nc.tensor.matmul_mx(out=bank[:], lhsT=got[True, i, j0].bitcast(FP8X4), lhsT_scale=got[False, i, j0],
                                 rhs=w_codes, rhs_scale=w_scales, start=True, stop=True)
             return bank[:]
 
-        h_tiles, h_q = {}, {}
-
-        def block_of(j0):
-            return [blk for blk in OUT_BLOCKS if blk[0] <= j0 < blk[0] + blk[1]][0]
-
-        def h_tile(block):
-            if block not in h_tiles:
-                if block[0] >= FOLDED_FROM:
-                    tile = shared.tile([P, 8 * block[1]], BF16, name="h_bf%d" % block[0], align_bytes=64,
-                                       offset=49152 + (4096 if block == EARLY_ROUNDED else 2048))
-                elif block == OUT_BLOCKS[2]:
-                    tile = shared.tile([P, 8 * block[1]], BF16, name="h_bf%d" % block[0], align_bytes=64, offset=0)
-                else:
-                    tile = keep.tile([P, 8 * block[1]], BF16, name="h_bf%d" % block[0], align_bytes=64)
-                h_tiles.setdefault(block, tile)
-            return h_tiles[block]
-
-        def h_slice(unit):
-            j0, b = unit
-            first, width = block_of(j0)
-            c0 = b * width + j0 - first
-            return h_tile((first, width))[:, 4 * c0 : 4 * (c0 + J)]
-
-        def block_slice(tiles, name, unit):
-            j0, b = unit
-            block = block_of(j0)
-            if block not in tiles and name == "other" and block == OUT_BLOCKS[5]:
-                tiles.setdefault(block, shared.tile([P, 8 * block[1]], BF16, name="other_late", align_bytes=64, offset=0))
-            if block not in tiles:
-                tiles.setdefault(block, keep.tile([P, 8 * block[1]], BF16, name="%s_bf%d" % (name, block[0]), align_bytes=64))
-            c0 = b * block[1] + j0 - block[0]
-            return tiles[block][:, 4 * c0 : 4 * (c0 + J)]
-
         def as_words(ap):
             return ap.rearrange("p (j t) -> p j t", t=4)
 
-        units = [(j0, b) for first, width in OUT_BLOCKS for b in range(2) for j0 in range(first, first + width, J)]
-        plain = [u for u in units if u[0] < FOLDED_FROM]
-        folded = [u for u in units if u[0] >= FOLDED_FROM]
-        narrow = folded[:NARROW]
-        sides, largers, others, rounded_sides = {}, {}, {}, {}
+        folded = [(j0, 0) for j0 in range(0, FOLD, J)]
+        opening = [(0, 1), (128, 1)]
+        turned = [(256, 1), (384, 1)]
+        middle = [(512, 1), (640, 1)]
+        closing = [(j0, b) for j0 in (768, 896) for b in range(2)]
+        sides, largers, centres, h, h_q = {}, {}, {}, {}, {}
+        firsts = {}
+        second_bf = keep.tile([P, 4 * FOLD], BF16, align_bytes=64)
 
-        def side_offset(unit):
-            return 8192 + 3072 * units.index(unit)
+        def side(unit, kb):
+            tile = at(kb, [P, 4 * J], F32, "side%d_%d" % unit)
+            if unit in turned:
+                nc.scalar.activation(tile[:], fill_turned(FIRST, unit), ACT.Copy)
+            else:
+                nc.scalar.activation(as_words(tile[:]), fill_bank((FIRST,), unit), ACT.Copy)
+            sides.setdefault(unit, tile)
 
-        def larger_offset(unit):
-            return 66560 + 2048 * units.index(unit)
+        def folded_first(unit):
+            nc.scalar.activation(as_words(firsts[unit]), fill_bank((FIRST, CENTRE), unit), ACT.Relu)
 
-        turned = plain[TURNED[0] : TURNED[1]]
-        centres = {}
+        def folded_second(unit):
+            nc.scalar.activation(as_words(second_bf[:, 4 * unit[0] : 4 * (unit[0] + J)]), fill_bank((SECOND, CENTRE), unit), ACT.Copy)
 
-        def stage_centre(unit):
-            centre = keep.tile([P, 4 * P], F32, name="centre%d_%d" % unit)
-            nc.scalar.activation(centre[:], fill_turned(CENTRE, unit), ACT.Copy)
-            centres.setdefault(unit, centre)
+        def larger(unit, kb=None):
+            if kb is None:
+                tile = keep.tile([P, 4 * J], F32, name="larger%d_%d" % unit, align_bytes=64)
+            else:
+                tile = at(kb, [P, 4 * J], F32, "larger%d_%d" % unit)
+            if unit in turned:
+                nc.vector.tensor_tensor(tile[:], fill_turned(SECOND, unit), sides[unit][:], ALU.max)
+            else:
+                nc.vector.tensor_tensor(as_words(tile[:]), fill_bank((SECOND,), unit), as_words(sides[unit][:]), ALU.max)
+            largers.setdefault(unit, tile)
 
-        def stage_turn(unit):
-            bank = psum2.tile([P, 4, J], F32, name="bank")
+        def centre(unit):
+            tile = keep.tile([P, 4 * P], F32, name="centre%d_%d" % unit)
+            nc.scalar.activation(tile[:], fill_turned(CENTRE, unit), ACT.Copy)
+            centres.setdefault(unit, tile)
+
+        def h_part(unit):
+            return h[unit]
+
+        def turn(unit):
+            bank = next_bank([P, 4, J])
             for t in range(4):
-                for n, term in enumerate((largers[unit], centres[unit])):
+                for n, term in enumerate((centres[unit], largers[unit])):
                     nc.tensor.matmul(bank[:, t, :], term[:, P * t : P * (t + 1)], identity[:], start=(n == 0), stop=(n == 1), is_transpose=True)
-            nc.scalar.activation(as_words(h_slice(unit)), bank[:].rearrange("p t j -> p j t"), ACT.Relu)
+            nc.scalar.activation(as_words(h_part(unit)), bank[:].rearrange("p t j -> p j t"), ACT.Relu)
 
-        def stage_side(unit):
-            if unit in turned:
-                side = shared.tile([P, 4 * J], F32, name="side%d_%d" % unit, align_bytes=64, offset=side_offset(unit))
-                nc.scalar.activation(side[:], fill_turned(FIRST, unit), ACT.Copy)
-                sides.setdefault(unit, side)
-                return
-            bank = fill_bank((CENTRE, FIRST) if unit in folded else (FIRST,), unit)
-            if unit in narrow:
-                nc.scalar.activation(as_words(block_slice(rounded_sides, "side", unit)), bank, ACT.Relu)
-                return
-            side = shared.tile([P, 4 * J], F32, name="side%d_%d" % unit, align_bytes=64, offset=side_offset(unit))
-            nc.scalar.activation(as_words(side[:]), bank, ACT.Relu if unit in folded else ACT.Copy)
-            sides.setdefault(unit, side)
+        def diff(unit):
+            nc.vector.tensor_tensor(as_words(h_part(unit)), fill_bank((CENTRE,), unit), as_words(largers[unit][:]), ALU.add)
 
-        def stage_other(unit):
-            bank = fill_bank((SECOND, CENTRE), unit)
-            nc.scalar.activation(as_words(block_slice(others, "other", unit)), bank, ACT.Copy)
-
-        def rounded_max(block):
-            nc.vector.tensor_tensor(h_tile(block)[:], others[block][:], rounded_sides[block][:], ALU.max)
-
-        def stage_max(unit):
-            if unit in turned:
-                larger = shared.tile([P, 4 * J], F32, name="larger%d_%d" % unit, align_bytes=64, offset=larger_offset(unit))
-                nc.vector.tensor_tensor(larger[:], fill_turned(SECOND, unit), sides[unit][:], ALU.max)
-                largers.setdefault(unit, larger)
-            elif unit in folded:
-                bank = fill_bank((CENTRE, SECOND), unit)
-                nc.vector.tensor_tensor(as_words(h_slice(unit)), bank, as_words(sides[unit][:]), ALU.max)
+        def relu(engine, ap):
+            if engine == "scalar":
+                nc.scalar.activation(ap, ap, ACT.Relu)
+            elif engine == "gpsimd":
+                nc.gpsimd.tensor_scalar(ap, ap, F32_MAX, 0.0, ALU.min, ALU.max)
             else:
-                bank = fill_bank((SECOND,), unit)
-                larger = shared.tile([P, 4 * J], F32, name="larger%d_%d" % unit, align_bytes=64, offset=larger_offset(unit))
-                nc.vector.tensor_tensor(as_words(larger[:]), bank, as_words(sides[unit][:]), ALU.max)
-                largers.setdefault(unit, larger)
+                nc.vector.tensor_scalar(ap, ap, 0.0, None, ALU.max)
 
-        def stage_diff(unit):
-            if unit in plain:
-                bank = fill_bank((CENTRE,), unit)
-                nc.vector.tensor_tensor(as_words(h_slice(unit)), bank, as_words(largers[unit][:]), ALU.add)
+        def place(table, tile, units):
+            for n, unit in enumerate(units):
+                table.setdefault(unit, tile[:, 4 * J * n : 4 * J * (n + 1)])
 
-        def stage_relu(unit):
-            if plain.index(unit) in ON_GPSIMD:
-                nc.gpsimd.tensor_scalar(h_slice(unit), h_slice(unit), F32_MAX, 0.0, ALU.min, ALU.max)
+        def quantize_h(src, units, kb=None):
+            width = J * len(units)
+            if kb is None:
+                codes = keep.tile([P, width], U32, name="h_q%d_%d" % units[0], align_bytes=64)
             else:
-                nc.scalar.activation(h_slice(unit), h_slice(unit), ACT.Relu)
-
-        def quantize_h(block, first_half=0, halves=2):
-            j0, width = block
-            lo, hi = first_half * width, (first_half + halves) * width
-            if block not in h_q:
-                if j0 == 0:
-                    h_q.setdefault(block, shared.tile([P, 2 * width], U32, name="h_q0", align_bytes=64, offset=side_offset(plain[6]) + 1024))
-                else:
-                    h_q.setdefault(block, keep.tile([P, 2 * width], U32, name="h_q%d" % j0, align_bytes=64))
-            nc.vector.quantize_mx(out=h_q[block][:, lo:hi].bitcast(FP8X4), scales=h_s[:, 2 * j0 + lo : 2 * j0 + hi],
-                                  in_=h_tile(block)[:, 4 * lo : 4 * hi])
+                codes = at(kb, [P, width], U32, "h_q%d_%d" % units[0])
+            scales = keep.tile([P, width], U8, name="h_s%d_%d" % units[0], align_bytes=64)
+            nc.vector.quantize_mx(out=codes[:].bitcast(FP8X4), scales=scales[:], in_=src)
+            for n, unit in enumerate(units):
+                h_q.setdefault(unit, (codes, scales, J * n))
 
         out_rows = out.rearrange("(t p) j -> p t j", p=P)
 
-        def second_layer(dst, nt, b, j0, width):
-            h_cols = slice(2 * j0 + b * width, 2 * j0 + (b + 1) * width)
-            nc.tensor.matmul_mx(out=dst, lhsT=wo_q[0][:, b, P * nt : P * (nt + 1)].bitcast(FP8X4), lhsT_scale=wo_s[:, b, P * nt : P * (nt + 1)],
-                                rhs=h_q[j0, width][:, b * width : (b + 1) * width].bitcast(FP8X4), rhs_scale=h_s[:, h_cols], start=(b == 0), stop=(b == 1))
+        def second_layer(dst, nt, b, blk):
+            j0, width = blk
+            codes, scales, c0 = h_q[j0, b]
+            nc.tensor.matmul_mx(out=dst, lhsT=wo_q[:, b, P * nt : P * (nt + 1)].bitcast(FP8X4), lhsT_scale=wo_s[:, b, P * nt : P * (nt + 1)],
+                                rhs=codes[:, c0 : c0 + width].bitcast(FP8X4), rhs_scale=scales[:, c0 : c0 + width], start=(b == 0), stop=(b == 1))
 
-        def output_block(j0, width):
+        def output(blk, rows, engine="scalar"):
+            j0, width = blk
             cols = slice(j0, j0 + width)
-            for pair in range(2):
-                bank = (psum2 if width == 256 else psum1).tile([P, 2, 256], F32, name="bank")
-                for e in range(2):
-                    for b in range(2):
-                        second_layer(bank[:, e, 0:width], 2 * pair + e, b, j0, width)
-                for e in range(2):
-                    nt = 2 * pair + e
-                    nc.scalar.activation(res[:, nt, cols], bank[:, e, 0:width], ACT.Relu, bias=bias[:, nt : nt + 1])
-                nc.sync.dma_start(out_rows[:, 2 * pair : 2 * pair + 2, cols], res[:, 2 * pair : 2 * pair + 2, cols])
-
-        def output_narrow(j0, width):
-            cols = slice(j0, j0 + width)
-            bank = psum2.tile([P, 4, J], F32, name="bank")
-            for nt in range(4):
+            bank = next_bank([P, len(rows), width])
+            for e, nt in enumerate(rows):
                 for b in range(2):
-                    second_layer(bank[:, nt, :], nt, b, j0, width)
-            for nt in range(4):
-                nc.scalar.activation(res[:, nt, cols], bank[:, nt, :], ACT.Relu, bias=bias[:, nt : nt + 1])
-            nc.sync.dma_start(out_rows[:, :, cols], res[:, :, cols])
-
-        def output_shared(j0, width):
-            cols = slice(j0, j0 + width)
-            for pair in range(2):
-                bank = psum2.tile([P, 2, J], F32, name="bank")
-                for e in range(2):
-                    for b in range(2):
-                        second_layer(bank[:, e, :], 2 * pair + e, b, j0, width)
-                for e in range(2):
-                    nt = 2 * pair + e
-                    if pair == 0:
-                        nc.vector.tensor_scalar(res[:, nt, cols], bank[:, e, :], bias[:, nt : nt + 1], 0.0, ALU.add, ALU.max)
-                    else:
-                        nc.scalar.activation(res[:, nt, cols], bank[:, e, :], ACT.Relu, bias=bias[:, nt : nt + 1])
-                nc.sync.dma_start(out_rows[:, 2 * pair : 2 * pair + 2, cols], res[:, 2 * pair : 2 * pair + 2, cols])
-
-        def output_last_block(j0, width):
-            cols = slice(j0, j0 + width)
-            banks = [psum1.tile([P, 2, 256], F32, name="bank") for nt in range(4)]
-            for b in range(2):
-                for nt in range(4):
-                    second_layer(banks[nt][:, 0, 0:width], nt, b, j0, width)
-            for nt in range(4):
-                if nt % 2 == 0:
-                    nc.vector.tensor_scalar(res[:, nt, cols], banks[nt][:, 0, 0:width], bias[:, nt : nt + 1], 0.0, ALU.add, ALU.max)
+                    second_layer(bank[:, e, :], nt, b, blk)
+            for e, nt in enumerate(rows):
+                if engine == "vector":
+                    nc.vector.tensor_scalar(res[:, nt, cols], bank[:, e, :], bias[:, nt : nt + 1], 0.0, ALU.add, ALU.max)
                 else:
-                    nc.scalar.activation(res[:, nt, cols], banks[nt][:, 0, 0:width], ACT.Relu, bias=bias[:, nt : nt + 1])
-                    nc.sync.dma_start(out_rows[:, nt - 1 : nt + 1, cols], res[:, nt - 1 : nt + 1, cols])
+                    nc.scalar.activation(res[:, nt, cols], bank[:, e, :], ACT.Relu, bias=bias[:, nt : nt + 1])
 
-        deal_columns(wa_q, wa_raw, 2)
-        gather_scales(FIRST)
-        gather(tab_w, U32, FIRST, 0, HEAD, keep.tile([P, HEAD], U32, name="got_w1_head", align_bytes=64))
-        deal_scales(wa_s, was_raw)
-        gather(tab_w, U32, FIRST, HEAD, S - HEAD, shared.tile([P, S - HEAD], U32, name="got_w1_rest", align_bytes=64, offset=5120))
-        gather_scales(CENTRE)
-        gather_words(CENTRE)
+        def store(blk, rows):
+            cols = slice(blk[0], blk[0] + blk[1])
+            nc.sync.dma_start(out_rows[:, rows[0] : rows[-1] + 1, cols], res[:, rows[0] : rows[-1] + 1, cols])
+
+        def finish(blk):
+            for rows in ((0, 1), (2, 3)) if blk[1] == 256 else ((0, 1, 2, 3),):
+                output(blk, rows)
+                store(blk, rows)
+
+        deal_columns(vector_move, wa_q, wa_raw, 2)
+        gather(tab_s, U8, FIRST, 0, S, keep.tile([P, S], U8, name="got_s1", align_bytes=64))
+        gather(tab_s, U8, CENTRE, 0, S, keep.tile([P, S], U8, name="got_s0", align_bytes=64))
+        gather(tab_w, U32, FIRST, 0, 256, keep.tile([P, 256], U32, name="got_w1_head", align_bytes=64))
+        gather(tab_w, U32, CENTRE, 0, 256, keep.tile([P, 256], U32, name="got_w0_head", align_bytes=64))
+        cast_wc(0)
+        wa_s = keep.tile([P, H // 4], I32, align_bytes=64)
+        wb_s = keep.tile([P, H // 4], I32, align_bytes=64)
+        wb_q = keep.tile([P, H], I32, align_bytes=64)
+        deal_scales(nc.scalar.copy, wa_s, was_raw)
+        deal_columns(nc.scalar.copy, wb_q, wb_raw, 4)
+        deal_scales(nc.scalar.copy, wb_s, wbs_raw)
         quantize_wc(0)
-        gather(tab_s, U8, SECOND, 0, S, shared.tile([P, S], U8, name="got_s2", align_bytes=64, offset=57344))
+        gather(tab_w, U32, FIRST, 256, 768, at(20, [P, 768], U32, "got_w1_rest"))
+        gather(tab_w, U32, CENTRE, 256, 512, at(23, [P, 512], U32, "got_w0_mid"))
+        gather(tab_s, U8, SECOND, 0, S, keep.tile([P, S], U8, name="got_s2", align_bytes=64))
+        gather(tab_w, U32, SECOND, 0, 512, keep.tile([P, 512], U32, name="got_w2_head", align_bytes=64))
+        first_head = at(25, [P, 1024], BF16, "first_head")
+        place(firsts, first_head, folded[:2])
+        side(opening[0], 27)
+        side(opening[1], 29)
+        folded_first(folded[0])
+        folded_first(folded[1])
+        cast_wc(1)
         quantize_wc(1)
-        deal_columns(wb_q, wb_raw, 4)
-        deal_scales(wb_s, wbs_raw)
-        gather(tab_w, U32, SECOND, 0, HEAD, shared.tile([P, HEAD], U32, name="got_w2_head", align_bytes=64, offset=61440))
-        gather(tab_w, U32, SECOND, HEAD, S - HEAD, shared.tile([P, S - HEAD], U32, name="got_w2_rest", align_bytes=64, offset=63488))
-        for unit in plain + [u for u in folded if u[1] == 0] + [u for u in folded if u[1] == 1]:
-            stage_side(unit)
-        cast_wo_on_gpsimd(0)
-        cast_wo_on_gpsimd(1)
-
-        def plain_step(n):
-            if n < len(plain):
-                stage_max(plain[n])
-            if 1 <= n <= len(plain):
-                stage_diff(plain[n - 1])
-            if 2 <= n and plain[n - 2] not in turned:
-                stage_relu(plain[n - 2])
-
-        reads = [(stage_other, u) for u in folded]
-        B0, C1, C2, C3, EARLY, LATE = OUT_BLOCKS
-        for n in range(5):
-            plain_step(n)
-            if n >= 1:
-                stage, unit = reads[n - 1]
-                stage(unit)
-        stage_max(plain[5])
-        stage_relu(plain[3])
-        stage, unit = reads[4]
-        stage(unit)
-        stage_max(plain[6])
-        for stage, unit in reads[5:]:
-            stage(unit)
-        for unit in turned:
-            stage_centre(unit)
-        for unit in turned:
-            stage_turn(unit)
-        quantize_wo(plain[5])
-        quantize_h(B0)
-        rounded_max(EARLY)
-        rounded_max(LATE)
-        quantize_h(EARLY)
-        quantize_h(LATE)
-        quantize_h(C1)
-        output_block(*B0)
-        output_block(*EARLY)
-        plain_step(7)
-        plain_step(8)
-        output_narrow(*LATE)
-        plain_step(9)
-        output_narrow(*C1)
-        quantize_h(C2)
-        plain_step(10)
-        plain_step(11)
-        quantize_h(C3, 0, 1)
-        output_shared(*C2)
-        quantize_h(C3, 1, 1)
-        output_last_block(*C3)
+        gather(tab_w, U32, CENTRE, 768, 256, at(31, [P, 256], U32, "got_w0_rest"))
+        gather(tab_w, U32, SECOND, 512, 512, keep.tile([P, 512], U32, name="got_w2_rest", align_bytes=64))
+        wo_bf = at(1, [P, 2, 4 * N], BF16, "wo_bf")
+        for b in range(2):
+            nc.gpsimd.tensor_scalar(wo_bf[:, b, :].rearrange("p (n t) -> p n t", t=4), wo_raw[b][:].rearrange("p t n -> p n t"),
+                                    1.0, 0.0, ALU.mult, ALU.add)
+        h_open = keep.tile([P, 1024], BF16, align_bytes=64)
+        h_turned = keep.tile([P, 1024], BF16, align_bytes=64)
+        h_middle = keep.tile([P, 1024], BF16, align_bytes=64)
+        h_last = [keep.tile([P, 1024], BF16, name="h_last%d" % n, align_bytes=64) for n in range(2)]
+        place(h, h_open, opening)
+        place(h, h_turned, turned)
+        place(h, h_middle, middle)
+        place(h, h_last[0], closing[:2])
+        place(h, h_last[1], closing[2:])
+        first_rest = at(32.5, [P, 2048], BF16, "first_rest")
+        place(firsts, first_rest, folded[2:])
+        side(turned[0], 36.5)
+        side(turned[1], 38.5)
+        for unit in folded[2:]:
+            folded_first(unit)
+        side(middle[0], 40.5)
+        side(middle[1], 42.5)
+        folded_second(folded[0])
+        larger(opening[0])
+        larger(opening[1])
+        folded_second(folded[1])
+        diff(opening[0])
+        folded_second(folded[2])
+        diff(opening[1])
+        folded_second(folded[3])
+        larger(turned[0])
+        larger(turned[1])
+        folded_second(folded[4])
+        larger(middle[0], 46)
+        folded_second(folded[5])
+        larger(middle[1])
+        centre(turned[0])
+        diff(middle[0])
+        centre(turned[1])
+        diff(middle[1])
+        wo_q = at(44.5, [P, 2, N], U32, "wo_q")
+        nc.vector.quantize_mx(out=wo_q[:].rearrange("p b n -> p (b n)").bitcast(FP8X4), scales=wo_s[:].rearrange("p b n -> p (b n)"),
+                              in_=wo_bf[:].rearrange("p b n -> p (b n)"))
+        relu("scalar", h_open[:])
+        turn(turned[0])
+        turn(turned[1])
+        for n in range(4):
+            side(closing[n], 50 + 2 * n)
+        h_head = at(1, [P, 1024], BF16, "h_head")
+        h_rest = at(3, [P, 2048], BF16, "h_rest")
+        relu("vector", h_middle[:])
+        nc.vector.tensor_tensor(h_head[:], second_bf[:, 0:1024], first_head[:], ALU.max)
+        quantize_h(h_open[:], opening, 7)
+        quantize_h(h_head[:], folded[:2])
+        nc.vector.tensor_tensor(h_rest[:], second_bf[:, 1024:3072], first_rest[:], ALU.max)
+        quantize_h(h_turned[:], turned, 8)
+        quantize_h(h_rest[:], folded[2:])
+        quantize_h(h_middle[:], middle)
+        larger(closing[0])
+        larger(closing[1])
+        finish(WIDE[0])
+        diff(closing[0])
+        diff(closing[1])
+        finish(WIDE[1])
+        relu("gpsimd", h[closing[0]])
+        larger(closing[2])
+        relu("gpsimd", h[closing[1]])
+        larger(closing[3])
+        diff(closing[2])
+        diff(closing[3])
+        finish(WIDE[2])
+        quantize_h(h_last[0][:], closing[:2])
+        relu("vector", h_last[1][:])
+        output(LAST[0], (0, 1), "vector")
+        store(LAST[0], (0, 1))
+        quantize_h(h_last[1][:], closing[2:])
+        output(LAST[0], (2, 3))
+        store(LAST[0], (2, 3))
+        output(LAST[1], (0, 1), "vector")
+        store(LAST[1], (0, 1))
+        output(LAST[1], (2, 3))
+        store(LAST[1], (2, 3))

@@ -84,10 +84,12 @@ def tile_list_point_edge_conv_kernel(tc, tab_words, tab_scales, offs, offs2, off
         nc.sync.dma_start(wc_raw[0][:], wc_rows[:, :, 0:512])
         nc.sync.dma_start(tab_w[:], tab_words[0].rearrange("p t i -> p (t i)").bitcast(I32))
         load_scales(was_raw, wa_scales)
-        nc.sync.dma_start(wb_raw[:], wb_words[0].rearrange("p e i -> p (e i)").bitcast(I32))
+        wb_rows = wb_words[0].rearrange("p e i -> p (e i)").bitcast(I32)
+        for b in range(2):
+            nc.sync.dma_start(wb_raw[:, 512 * b : 512 * (b + 1)], wb_rows[:, 512 * b : 512 * (b + 1)])
         nc.sync.dma_start(lists[SECOND][:], offs3)
-        load_scales(wbs_raw, wb_scales)
         nc.sync.dma_start(wc_raw[1][:], wc_rows[:, :, 512:1024])
+        load_scales(wbs_raw, wb_scales)
         load_wo(0)
         load_wo(1)
         with nc.allow_non_contiguous_dma(reason="one bias value a partition"):
@@ -98,14 +100,18 @@ def tile_list_point_edge_conv_kernel(tc, tab_words, tab_scales, offs, offs2, off
         def gather(window, dtype, i, first, count, dst):
             nc.vector.tensor_copy(dst[:], window[:].bitcast(dtype).indirect(lists[i][:, first // 16 : (first + count) // 16]))
             for j0 in range(first, first + count, J):
-                got.setdefault((dtype == U32, i, j0), dst[:, j0 - first : j0 - first + J])
+                got.setdefault((dtype == U32, i, j0), (dst, j0 - first))
+
+        def picked(i, j0, n):
+            (words, c0), (scales, d0) = got[True, i, j0], got[False, i, j0]
+            return words[:, c0 : c0 + n].bitcast(FP8X4), scales[:, d0 : d0 + n]
 
         def vector_move(dst, src):
             nc.vector.tensor_copy(dst.bitcast(I32), src.bitcast(I32))
 
         def deal_columns(move, dst, src, run):
-            move(dst[:].bitcast(U32).rearrange("p (b t u s) -> p b t u s", b=2, t=4, s=run),
-                 src[:].bitcast(U32).rearrange("p (b u t s) -> p b t u s", b=2, t=4, s=run))
+            move(dst.bitcast(U32).rearrange("p (b t u s) -> p b t u s", u=32, t=4, s=run),
+                 src.bitcast(U32).rearrange("p (b u t s) -> p b t u s", u=32, t=4, s=run))
 
         def deal_scales(move, dst, src):
             move(dst[:].bitcast(U32).rearrange("p (b t g u) -> p b g t u", b=2, t=4, u=4),
@@ -128,121 +134,138 @@ def tile_list_point_edge_conv_kernel(tc, tab_words, tab_scales, offs, offs2, off
             return wb_q[:, col : col + n].bitcast(FP8X4), wb_s[:].bitcast(U8)[:, col : col + n]
 
         def fill_bank(terms, unit):
-            j0, b = unit
-            bank = next_bank([P, 4, J])
-            for t in range(4):
+            j0, b = unit[:2]
+            slots, width = (range(4), J) if len(unit) == 2 else ((2 * unit[2], 2 * unit[2] + 1), 2 * J)
+            bank = next_bank([P, len(slots), width])
+            for e, t in enumerate(slots):
                 for n, i in enumerate(terms):
                     w_codes, w_scales = weights(i, 512 * b + P * t)
-                    nc.tensor.matmul_mx(out=bank[:, t, :], lhsT=w_codes, lhsT_scale=w_scales, rhs=got[True, i, j0].bitcast(FP8X4),
-                                        rhs_scale=got[False, i, j0], start=(n == 0), stop=(n == len(terms) - 1))
+                    v_codes, v_scales = picked(i, j0, width)
+                    nc.tensor.matmul_mx(out=bank[:, e, :], lhsT=w_codes, lhsT_scale=w_scales, rhs=v_codes, rhs_scale=v_scales,
+                                        start=(n == 0), stop=(n == len(terms) - 1))
             return bank[:].rearrange("p t j -> p j t")
 
         def fill_turned(i, unit):
             j0, b = unit
             bank = next_bank([P, 4 * P])
             w_codes, w_scales = weights(i, 512 * b, 512)
-            nc.tensor.matmul_mx(out=bank[:], lhsT=got[True, i, j0].bitcast(FP8X4), lhsT_scale=got[False, i, j0],
-                                rhs=w_codes, rhs_scale=w_scales, start=True, stop=True)
+            v_codes, v_scales = picked(i, j0, J)
+            nc.tensor.matmul_mx(out=bank[:], lhsT=v_codes, lhsT_scale=v_scales, rhs=w_codes, rhs_scale=w_scales, start=True, stop=True)
             return bank[:]
 
-        def as_words(ap):
-            return ap.rearrange("p (j t) -> p j t", t=4)
+        def as_words(ap, unit):
+            return ap.rearrange("p (j t) -> p j t", t=4 if len(unit) == 2 else 2)
 
-        folded = [(j0, 0) for j0 in range(0, FOLD, J)]
-        opening = [(0, 1), (128, 1)]
+        def joined(ap):
+            return ap.rearrange("p (j g e) -> p j g e", g=2, e=2)
+
+        def parted(ap):
+            return ap.rearrange("p (g j e) -> p j g e", g=2, e=2)
+
+        folded = [(j0, 0, g) for j0 in range(0, FOLD, 2 * J) for g in range(2)]
+        opening = [(0, 1, 0), (0, 1, 1)]
         turned = [(256, 1), (384, 1)]
-        middle = [(512, 1), (640, 1)]
+        middle = [(512, 1, 0), (512, 1, 1)]
         closing = [(j0, b) for j0 in (768, 896) for b in range(2)]
         sides, largers, centres, h, h_q = {}, {}, {}, {}, {}
-        firsts = {}
-        second_bf = keep.tile([P, 4 * FOLD], BF16, align_bytes=64)
+        firsts, seconds = {}, {}
 
         def side(unit, kb):
-            tile = at(kb, [P, 4 * J], F32, "side%d_%d" % unit)
+            tile = at(kb, [P, 4 * J], F32, "side%d_%d" % (unit[0], sum(unit[1:])))
             if unit in turned:
                 nc.scalar.activation(tile[:], fill_turned(FIRST, unit), ACT.Copy)
             else:
-                nc.scalar.activation(as_words(tile[:]), fill_bank((FIRST,), unit), ACT.Copy)
+                nc.scalar.activation(as_words(tile[:], unit), fill_bank((FIRST,), unit), ACT.Copy)
             sides.setdefault(unit, tile)
 
         def folded_first(unit):
-            nc.scalar.activation(as_words(firsts[unit]), fill_bank((FIRST, CENTRE), unit), ACT.Relu)
+            nc.scalar.activation(as_words(firsts[unit], unit), fill_bank((FIRST, CENTRE), unit), ACT.Relu)
 
         def folded_second(unit):
-            nc.scalar.activation(as_words(second_bf[:, 4 * unit[0] : 4 * (unit[0] + J)]), fill_bank((SECOND, CENTRE), unit), ACT.Copy)
+            nc.scalar.activation(as_words(seconds[unit], unit), fill_bank((SECOND, CENTRE), unit), ACT.Copy)
 
         def larger(unit, kb=None):
             if kb is None:
-                tile = keep.tile([P, 4 * J], F32, name="larger%d_%d" % unit, align_bytes=64)
+                tile = keep.tile([P, 4 * J], F32, name="larger%d_%d" % (unit[0], sum(unit[1:])), align_bytes=64)
             else:
-                tile = at(kb, [P, 4 * J], F32, "larger%d_%d" % unit)
+                tile = at(kb, [P, 4 * J], F32, "larger%d_%d" % (unit[0], sum(unit[1:])))
             if unit in turned:
                 nc.vector.tensor_tensor(tile[:], fill_turned(SECOND, unit), sides[unit][:], ALU.max)
             else:
-                nc.vector.tensor_tensor(as_words(tile[:]), fill_bank((SECOND,), unit), as_words(sides[unit][:]), ALU.max)
+                nc.vector.tensor_tensor(as_words(tile[:], unit), fill_bank((SECOND,), unit), as_words(sides[unit][:], unit), ALU.max)
             largers.setdefault(unit, tile)
 
         def centre(unit):
-            tile = keep.tile([P, 4 * P], F32, name="centre%d_%d" % unit)
+            tile = keep.tile([P, 4 * P], F32, name="centre%d_%d" % (unit[0], sum(unit[1:])))
             nc.scalar.activation(tile[:], fill_turned(CENTRE, unit), ACT.Copy)
             centres.setdefault(unit, tile)
-
-        def h_part(unit):
-            return h[unit]
 
         def turn(unit):
             bank = next_bank([P, 4, J])
             for t in range(4):
                 for n, term in enumerate((centres[unit], largers[unit])):
                     nc.tensor.matmul(bank[:, t, :], term[:, P * t : P * (t + 1)], identity[:], start=(n == 0), stop=(n == 1), is_transpose=True)
-            nc.scalar.activation(as_words(h_part(unit)), bank[:].rearrange("p t j -> p j t"), ACT.Relu)
+            nc.scalar.activation(as_words(h[unit], unit), bank[:].rearrange("p t j -> p j t"), ACT.Relu)
 
         def diff(unit):
-            nc.vector.tensor_tensor(as_words(h_part(unit)), fill_bank((CENTRE,), unit), as_words(largers[unit][:]), ALU.add)
+            nc.vector.tensor_tensor(as_words(h[unit], unit), fill_bank((CENTRE,), unit), as_words(largers[unit][:], unit), ALU.add)
 
-        def relu(engine, ap):
+        def relu(engine, dst, src):
             if engine == "scalar":
-                nc.scalar.activation(ap, ap, ACT.Relu)
+                nc.scalar.activation(dst, src, ACT.Relu)
             elif engine == "gpsimd":
-                nc.gpsimd.tensor_scalar(ap, ap, F32_MAX, 0.0, ALU.min, ALU.max)
+                nc.gpsimd.tensor_scalar(dst, src, F32_MAX, 0.0, ALU.min, ALU.max)
             else:
-                nc.vector.tensor_scalar(ap, ap, 0.0, None, ALU.max)
+                nc.vector.tensor_scalar(dst, src, 0.0, None, ALU.max)
 
         def place(table, tile, units):
             for n, unit in enumerate(units):
                 table.setdefault(unit, tile[:, 4 * J * n : 4 * J * (n + 1)])
 
-        def quantize_h(src, units, kb=None):
-            width = J * len(units)
+        def place_parted(table, tile, units):
+            half = 2 * J * len(units)
+            for unit in units:
+                c0 = half * unit[2] + 2 * (unit[0] - units[0][0])
+                table.setdefault(unit, tile[:, c0 : c0 + 4 * J])
+
+        def quantize_h(src, starts, kb=None):
+            width = src.shape[1] // 4
             if kb is None:
-                codes = keep.tile([P, width], U32, name="h_q%d_%d" % units[0], align_bytes=64)
+                codes = keep.tile([P, width], U32, name="h_q%d_%d" % starts[0], align_bytes=64)
             else:
-                codes = at(kb, [P, width], U32, "h_q%d_%d" % units[0])
-            scales = keep.tile([P, width], U8, name="h_s%d_%d" % units[0], align_bytes=64)
+                codes = at(kb, [P, width], U32, "h_q%d_%d" % starts[0])
+            scales = keep.tile([P, width], U8, name="h_s%d_%d" % starts[0], align_bytes=64)
             nc.vector.quantize_mx(out=codes[:].bitcast(FP8X4), scales=scales[:], in_=src)
-            for n, unit in enumerate(units):
-                h_q.setdefault(unit, (codes, scales, J * n))
+            for n, start in enumerate(starts):
+                h_q.setdefault(start, (codes, scales, width // len(starts) * n))
 
         out_rows = out.rearrange("(t p) j -> p t j", p=P)
 
-        def second_layer(dst, nt, b, blk):
+        def second_layer(dst, nt, b, blk, flags=None):
             j0, width = blk
             codes, scales, c0 = h_q[j0, b]
+            opens, closes = flags or (b == 0, b == 1)
             nc.tensor.matmul_mx(out=dst, lhsT=wo_q[:, b, P * nt : P * (nt + 1)].bitcast(FP8X4), lhsT_scale=wo_s[:, b, P * nt : P * (nt + 1)],
-                                rhs=codes[:, c0 : c0 + width].bitcast(FP8X4), rhs_scale=scales[:, c0 : c0 + width], start=(b == 0), stop=(b == 1))
+                                rhs=codes[:, c0 : c0 + width].bitcast(FP8X4), rhs_scale=scales[:, c0 : c0 + width], start=opens, stop=closes)
 
-        def output(blk, rows, engine="scalar"):
-            j0, width = blk
-            cols = slice(j0, j0 + width)
-            bank = next_bank([P, len(rows), width])
-            for e, nt in enumerate(rows):
-                for b in range(2):
-                    second_layer(bank[:, e, :], nt, b, blk)
+        def read_out(bank, blk, rows, engine):
+            cols = slice(blk[0], blk[0] + blk[1])
             for e, nt in enumerate(rows):
                 if engine == "vector":
                     nc.vector.tensor_scalar(res[:, nt, cols], bank[:, e, :], bias[:, nt : nt + 1], 0.0, ALU.add, ALU.max)
                 else:
                     nc.scalar.activation(res[:, nt, cols], bank[:, e, :], ACT.Relu, bias=bias[:, nt : nt + 1])
+
+        def output(blk, rows, engine="scalar"):
+            bank = next_bank([P, len(rows), blk[1]])
+            for e, nt in enumerate(rows):
+                for b in range(2):
+                    second_layer(bank[:, e, :], nt, b, blk)
+            read_out(bank, blk, rows, engine)
+
+        def half_pass(banks, blk, b):
+            for nt in range(4):
+                second_layer(banks[nt // 2][:, nt % 2, :], nt, b, blk, (b == 0 and nt % 2 == 0, b == 1 and nt % 2 == 1))
 
         def store(blk, rows):
             cols = slice(blk[0], blk[0] + blk[1])
@@ -253,30 +276,31 @@ def tile_list_point_edge_conv_kernel(tc, tab_words, tab_scales, offs, offs2, off
                 output(blk, rows)
                 store(blk, rows)
 
-        deal_columns(vector_move, wa_q, wa_raw, 2)
+        deal_columns(vector_move, wa_q[:], wa_raw[:], 2)
         gather(tab_s, U8, FIRST, 0, S, keep.tile([P, S], U8, name="got_s1", align_bytes=64))
         gather(tab_s, U8, CENTRE, 0, S, keep.tile([P, S], U8, name="got_s0", align_bytes=64))
         gather(tab_w, U32, FIRST, 0, 256, keep.tile([P, 256], U32, name="got_w1_head", align_bytes=64))
-        gather(tab_w, U32, CENTRE, 0, 256, keep.tile([P, 256], U32, name="got_w0_head", align_bytes=64))
         cast_wc(0)
         wa_s = keep.tile([P, H // 4], I32, align_bytes=64)
         wb_s = keep.tile([P, H // 4], I32, align_bytes=64)
         wb_q = keep.tile([P, H], I32, align_bytes=64)
         deal_scales(nc.scalar.copy, wa_s, was_raw)
-        deal_columns(nc.scalar.copy, wb_q, wb_raw, 4)
-        deal_scales(nc.scalar.copy, wb_s, wbs_raw)
+        for b in range(2):
+            deal_columns(nc.scalar.copy, wb_q[:, 512 * b : 512 * (b + 1)], wb_raw[:, 512 * b : 512 * (b + 1)], 4)
         quantize_wc(0)
+        gather(tab_w, U32, CENTRE, 0, 256, at(12, [P, 256], U32, "got_w0_head"))
         gather(tab_w, U32, FIRST, 256, 768, at(20, [P, 768], U32, "got_w1_rest"))
         gather(tab_w, U32, CENTRE, 256, 512, at(23, [P, 512], U32, "got_w0_mid"))
         gather(tab_s, U8, SECOND, 0, S, keep.tile([P, S], U8, name="got_s2", align_bytes=64))
         gather(tab_w, U32, SECOND, 0, 512, keep.tile([P, 512], U32, name="got_w2_head", align_bytes=64))
         first_head = at(25, [P, 1024], BF16, "first_head")
-        place(firsts, first_head, folded[:2])
+        place_parted(firsts, first_head, folded[:2])
         side(opening[0], 27)
         side(opening[1], 29)
         folded_first(folded[0])
         folded_first(folded[1])
         cast_wc(1)
+        deal_scales(nc.scalar.copy, wb_s, wbs_raw)
         quantize_wc(1)
         gather(tab_w, U32, CENTRE, 768, 256, at(31, [P, 256], U32, "got_w0_rest"))
         gather(tab_w, U32, SECOND, 512, 512, keep.tile([P, 512], U32, name="got_w2_rest", align_bytes=64))
@@ -288,13 +312,19 @@ def tile_list_point_edge_conv_kernel(tc, tab_words, tab_scales, offs, offs2, off
         h_turned = keep.tile([P, 1024], BF16, align_bytes=64)
         h_middle = keep.tile([P, 1024], BF16, align_bytes=64)
         h_last = [keep.tile([P, 1024], BF16, name="h_last%d" % n, align_bytes=64) for n in range(2)]
-        place(h, h_open, opening)
+        d_open = keep.tile([P, 1024], BF16, align_bytes=64)
+        d_middle = keep.tile([P, 1024], BF16, align_bytes=64)
+        place(h, d_open, opening)
         place(h, h_turned, turned)
-        place(h, h_middle, middle)
+        place(h, d_middle, middle)
         place(h, h_last[0], closing[:2])
         place(h, h_last[1], closing[2:])
         first_rest = at(32.5, [P, 2048], BF16, "first_rest")
-        place(firsts, first_rest, folded[2:])
+        place_parted(firsts, first_rest, folded[2:])
+        second_head = keep.tile([P, 1024], BF16, align_bytes=64)
+        second_rest = keep.tile([P, 2048], BF16, align_bytes=64)
+        place_parted(seconds, second_head, folded[:2])
+        place_parted(seconds, second_rest, folded[2:])
         side(turned[0], 36.5)
         side(turned[1], 38.5)
         for unit in folded[2:]:
@@ -322,42 +352,46 @@ def tile_list_point_edge_conv_kernel(tc, tab_words, tab_scales, offs, offs2, off
         wo_q = at(44.5, [P, 2, N], U32, "wo_q")
         nc.vector.quantize_mx(out=wo_q[:].rearrange("p b n -> p (b n)").bitcast(FP8X4), scales=wo_s[:].rearrange("p b n -> p (b n)"),
                               in_=wo_bf[:].rearrange("p b n -> p (b n)"))
-        relu("scalar", h_open[:])
+        relu("scalar", joined(h_open[:]), parted(d_open[:]))
         turn(turned[0])
         turn(turned[1])
         for n in range(4):
             side(closing[n], 50 + 2 * n)
         h_head = at(1, [P, 1024], BF16, "h_head")
         h_rest = at(3, [P, 2048], BF16, "h_rest")
-        relu("vector", h_middle[:])
-        nc.vector.tensor_tensor(h_head[:], second_bf[:, 0:1024], first_head[:], ALU.max)
-        quantize_h(h_open[:], opening, 7)
-        quantize_h(h_head[:], folded[:2])
-        nc.vector.tensor_tensor(h_rest[:], second_bf[:, 1024:3072], first_rest[:], ALU.max)
-        quantize_h(h_turned[:], turned, 8)
-        quantize_h(h_rest[:], folded[2:])
-        quantize_h(h_middle[:], middle)
+        relu("vector", joined(h_middle[:]), parted(d_middle[:]))
+        nc.vector.tensor_tensor(joined(h_head[:]), parted(second_head[:]), parted(first_head[:]), ALU.max)
+        quantize_h(h_open[:], [(0, 1)], 7)
+        quantize_h(h_head[:], [(0, 0)])
+        nc.vector.tensor_tensor(joined(h_rest[:]), parted(second_rest[:]), parted(first_rest[:]), ALU.max)
+        quantize_h(h_turned[:], [(256, 1)], 8)
+        quantize_h(h_rest[:], [(256, 0), (512, 0)])
+        quantize_h(h_middle[:], [(512, 1)])
         larger(closing[0])
         larger(closing[1])
         finish(WIDE[0])
         diff(closing[0])
         diff(closing[1])
         finish(WIDE[1])
-        relu("gpsimd", h[closing[0]])
+        relu("gpsimd", h[closing[0]], h[closing[0]])
         larger(closing[2])
-        relu("gpsimd", h[closing[1]])
+        relu("gpsimd", h[closing[1]], h[closing[1]])
         larger(closing[3])
         diff(closing[2])
+        quantize_h(h_last[0][:], closing[:2])
+        relu("gpsimd", h[closing[2]], h[closing[2]])
         diff(closing[3])
         finish(WIDE[2])
-        quantize_h(h_last[0][:], closing[:2])
-        relu("vector", h_last[1][:])
-        output(LAST[0], (0, 1), "vector")
+        output(LAST[0], (0, 1))
         store(LAST[0], (0, 1))
-        quantize_h(h_last[1][:], closing[2:])
+        relu("vector", h[closing[3]], h[closing[3]])
+        quantize_h(h[closing[2]], closing[2:3])
+        quantize_h(h[closing[3]], closing[3:])
         output(LAST[0], (2, 3))
         store(LAST[0], (2, 3))
-        output(LAST[1], (0, 1), "vector")
-        store(LAST[1], (0, 1))
-        output(LAST[1], (2, 3))
-        store(LAST[1], (2, 3))
+        banks = [next_bank([P, 2, J]) for n in range(2)]
+        for b in range(2):
+            half_pass(banks, LAST[1], b)
+        for n, engine in enumerate(("vector", "scalar")):
+            read_out(banks[n], LAST[1], (2 * n, 2 * n + 1), engine)
+            store(LAST[1], (2 * n, 2 * n + 1))

@@ -222,11 +222,10 @@ def tile_list_point_edge_conv_kernel(tc, tab_words, tab_scales, offs, offs2, off
             for n, unit in enumerate(units):
                 table.setdefault(unit, tile[:, 4 * J * n : 4 * J * (n + 1)])
 
-        def place_parted(table, tile, units):
-            half = 2 * J * len(units)
-            for unit in units:
-                c0 = half * unit[2] + 2 * (unit[0] - units[0][0])
-                table.setdefault(unit, tile[:, c0 : c0 + 4 * J])
+        def folded_max(dst, n):
+            cols = slice(1024 * n, 1024 * (n + 1))
+            first = first_head[:] if n == 0 else first_rest[:, 1024 * (n - 1) : 1024 * n]
+            nc.vector.tensor_tensor(joined(dst[:, 0:1024]), parted(second_bf[:, cols]), parted(first), ALU.max)
 
         def quantize_h(src, starts, kb=None):
             width = src.shape[1] // 4
@@ -241,12 +240,11 @@ def tile_list_point_edge_conv_kernel(tc, tab_words, tab_scales, offs, offs2, off
 
         out_rows = out.rearrange("(t p) j -> p t j", p=P)
 
-        def second_layer(dst, nt, b, blk, flags=None):
+        def second_layer(dst, nt, b, blk):
             j0, width = blk
             codes, scales, c0 = h_q[j0, b]
-            opens, closes = flags or (b == 0, b == 1)
             nc.tensor.matmul_mx(out=dst, lhsT=wo_q[:, b, P * nt : P * (nt + 1)].bitcast(FP8X4), lhsT_scale=wo_s[:, b, P * nt : P * (nt + 1)],
-                                rhs=codes[:, c0 : c0 + width].bitcast(FP8X4), rhs_scale=scales[:, c0 : c0 + width], start=opens, stop=closes)
+                                rhs=codes[:, c0 : c0 + width].bitcast(FP8X4), rhs_scale=scales[:, c0 : c0 + width], start=(b == 0), stop=(b == 1))
 
         def read_out(bank, blk, rows, engine):
             cols = slice(blk[0], blk[0] + blk[1])
@@ -265,7 +263,7 @@ def tile_list_point_edge_conv_kernel(tc, tab_words, tab_scales, offs, offs2, off
 
         def half_pass(banks, blk, b):
             for nt in range(4):
-                second_layer(banks[nt // 2][:, nt % 2, :], nt, b, blk, (b == 0 and nt % 2 == 0, b == 1 and nt % 2 == 1))
+                second_layer(banks[nt][:, 0, :], nt, b, blk)
 
         def store(blk, rows):
             cols = slice(blk[0], blk[0] + blk[1])
@@ -294,7 +292,7 @@ def tile_list_point_edge_conv_kernel(tc, tab_words, tab_scales, offs, offs2, off
         gather(tab_s, U8, SECOND, 0, S, keep.tile([P, S], U8, name="got_s2", align_bytes=64))
         gather(tab_w, U32, SECOND, 0, 512, keep.tile([P, 512], U32, name="got_w2_head", align_bytes=64))
         first_head = at(25, [P, 1024], BF16, "first_head")
-        place_parted(firsts, first_head, folded[:2])
+        place(firsts, first_head, folded[:2])
         side(opening[0], 27)
         side(opening[1], 29)
         folded_first(folded[0])
@@ -308,23 +306,17 @@ def tile_list_point_edge_conv_kernel(tc, tab_words, tab_scales, offs, offs2, off
         for b in range(2):
             nc.gpsimd.tensor_scalar(wo_bf[:, b, :].rearrange("p (n t) -> p n t", t=4), wo_raw[b][:].rearrange("p t n -> p n t"),
                                     1.0, 0.0, ALU.mult, ALU.add)
-        h_open = keep.tile([P, 1024], BF16, align_bytes=64)
-        h_turned = keep.tile([P, 1024], BF16, align_bytes=64)
-        h_middle = keep.tile([P, 1024], BF16, align_bytes=64)
-        h_last = [keep.tile([P, 1024], BF16, name="h_last%d" % n, align_bytes=64) for n in range(2)]
         d_open = keep.tile([P, 1024], BF16, align_bytes=64)
         d_middle = keep.tile([P, 1024], BF16, align_bytes=64)
+        h_last = [keep.tile([P, 1024], BF16, name="h_last%d" % n, align_bytes=64) for n in range(2)]
         place(h, d_open, opening)
-        place(h, h_turned, turned)
         place(h, d_middle, middle)
         place(h, h_last[0], closing[:2])
         place(h, h_last[1], closing[2:])
         first_rest = at(32.5, [P, 2048], BF16, "first_rest")
-        place_parted(firsts, first_rest, folded[2:])
-        second_head = keep.tile([P, 1024], BF16, align_bytes=64)
-        second_rest = keep.tile([P, 2048], BF16, align_bytes=64)
-        place_parted(seconds, second_head, folded[:2])
-        place_parted(seconds, second_rest, folded[2:])
+        place(firsts, first_rest, folded[2:])
+        second_bf = keep.tile([P, 3072], BF16, align_bytes=64)
+        place(seconds, second_bf, folded)
         side(turned[0], 36.5)
         side(turned[1], 38.5)
         for unit in folded[2:]:
@@ -341,57 +333,57 @@ def tile_list_point_edge_conv_kernel(tc, tab_words, tab_scales, offs, offs2, off
         folded_second(folded[3])
         larger(turned[0])
         larger(turned[1])
-        folded_second(folded[4])
-        larger(middle[0], 46)
-        folded_second(folded[5])
-        larger(middle[1])
+        side(closing[0], 52)
+        larger(middle[0], 63.5)
         centre(turned[0])
-        diff(middle[0])
+        larger(middle[1], 48)
         centre(turned[1])
+        diff(middle[0])
+        folded_second(folded[4])
         diff(middle[1])
+        larger(closing[0])
+        folded_second(folded[5])
         wo_q = at(44.5, [P, 2, N], U32, "wo_q")
         nc.vector.quantize_mx(out=wo_q[:].rearrange("p b n -> p (b n)").bitcast(FP8X4), scales=wo_s[:].rearrange("p b n -> p (b n)"),
                               in_=wo_bf[:].rearrange("p b n -> p (b n)"))
-        relu("scalar", joined(h_open[:]), parted(d_open[:]))
+        h_wide = [at(kb, [P, 2048], BF16, "h_wide%d" % n) for n, kb in enumerate((60, 65, 1))]
+        place(h, h_wide[1][:, 1024:2048], turned)
+        relu("scalar", joined(h_wide[0][:, 1024:2048]), parted(d_open[:]))
         turn(turned[0])
         turn(turned[1])
-        for n in range(4):
-            side(closing[n], 50 + 2 * n)
-        h_head = at(1, [P, 1024], BF16, "h_head")
-        h_rest = at(3, [P, 2048], BF16, "h_rest")
-        relu("vector", joined(h_middle[:]), parted(d_middle[:]))
-        nc.vector.tensor_tensor(joined(h_head[:]), parted(second_head[:]), parted(first_head[:]), ALU.max)
-        quantize_h(h_open[:], [(0, 1)], 7)
-        quantize_h(h_head[:], [(0, 0)])
-        nc.vector.tensor_tensor(joined(h_rest[:]), parted(second_rest[:]), parted(first_rest[:]), ALU.max)
-        quantize_h(h_turned[:], [(256, 1)], 8)
-        quantize_h(h_rest[:], [(256, 0), (512, 0)])
-        quantize_h(h_middle[:], [(512, 1)])
-        larger(closing[0])
+        for n in range(1, 4):
+            side(closing[n], 52 + 2 * n)
+        folded_max(h_wide[0], 0)
+        folded_max(h_wide[1], 1)
+        quantize_h(h_wide[0][:], [(0, 0), (0, 1)])
+        folded_max(h_wide[2], 2)
+        quantize_h(h_wide[1][:], [(256, 0), (256, 1)])
+        relu("vector", joined(h_wide[2][:, 1024:2048]), parted(d_middle[:]))
         larger(closing[1])
-        finish(WIDE[0])
+        quantize_h(h_wide[2][:], [(512, 0), (512, 1)])
         diff(closing[0])
-        diff(closing[1])
-        finish(WIDE[1])
+        finish(WIDE[0])
         relu("gpsimd", h[closing[0]], h[closing[0]])
-        larger(closing[2])
+        diff(closing[1])
         relu("gpsimd", h[closing[1]], h[closing[1]])
+        larger(closing[2])
+        finish(WIDE[1])
         larger(closing[3])
         diff(closing[2])
         quantize_h(h_last[0][:], closing[:2])
         relu("gpsimd", h[closing[2]], h[closing[2]])
         diff(closing[3])
         finish(WIDE[2])
-        output(LAST[0], (0, 1))
-        store(LAST[0], (0, 1))
+        for rows in ((0, 1), (2, 3)):
+            output(LAST[0], rows)
+            store(LAST[0], rows)
         relu("vector", h[closing[3]], h[closing[3]])
         quantize_h(h[closing[2]], closing[2:3])
         quantize_h(h[closing[3]], closing[3:])
-        output(LAST[0], (2, 3))
-        store(LAST[0], (2, 3))
-        banks = [next_bank([P, 2, J]) for n in range(2)]
+        banks = [next_bank([P, 1, J]) for nt in range(4)]
         for b in range(2):
             half_pass(banks, LAST[1], b)
-        for n, engine in enumerate(("vector", "scalar")):
-            read_out(banks[n], LAST[1], (2 * n, 2 * n + 1), engine)
-            store(LAST[1], (2 * n, 2 * n + 1))
+        for nt in range(4):
+            read_out(banks[nt], LAST[1], (nt,), ("vector", "scalar")[nt % 2])
+            if nt % 2:
+                store(LAST[1], (nt - 1, nt))

@@ -342,7 +342,6 @@ def tile_list_point_edge_conv_kernel(tc, tab_words, tab_scales, offs, offs2, off
         folded_second(folded[4])
         diff(middle[1])
         larger(closing[0])
-        folded_second(folded[5])
         wo_q = at(44.5, [P, 2, N], U32, "wo_q")
         nc.vector.quantize_mx(out=wo_q[:].rearrange("p b n -> p (b n)").bitcast(FP8X4), scales=wo_s[:].rearrange("p b n -> p (b n)"),
                               in_=wo_bf[:].rearrange("p b n -> p (b n)"))
@@ -350,21 +349,23 @@ def tile_list_point_edge_conv_kernel(tc, tab_words, tab_scales, offs, offs2, off
         place(h, h_wide[1][:, 1024:2048], turned)
         relu("scalar", joined(h_wide[0][:, 1024:2048]), parted(d_open[:]))
         turn(turned[0])
+        folded_second(folded[5])
+        side(closing[1], 54)
         turn(turned[1])
-        for n in range(1, 4):
-            side(closing[n], 52 + 2 * n)
+        relu("scalar", joined(h_wide[2][:, 1024:2048]), parted(d_middle[:]))
+        side(closing[2], 56)
+        side(closing[3], 58)
         folded_max(h_wide[0], 0)
         folded_max(h_wide[1], 1)
         quantize_h(h_wide[0][:], [(0, 0), (0, 1)])
         folded_max(h_wide[2], 2)
         quantize_h(h_wide[1][:], [(256, 0), (256, 1)])
-        relu("vector", joined(h_wide[2][:, 1024:2048]), parted(d_middle[:]))
         larger(closing[1])
         quantize_h(h_wide[2][:], [(512, 0), (512, 1)])
         diff(closing[0])
+        diff(closing[1])
         finish(WIDE[0])
         relu("gpsimd", h[closing[0]], h[closing[0]])
-        diff(closing[1])
         relu("gpsimd", h[closing[1]], h[closing[1]])
         larger(closing[2])
         finish(WIDE[1])

@@ -372,14 +372,14 @@ def tile_list_point_edge_conv_kernel(tc, tab_words, tab_scales, offs, offs2, off
         larger(closing[3])
         diff(closing[2])
         quantize_h(h_last[0][:], closing[:2])
-        relu("gpsimd", h[closing[2]], h[closing[2]])
+        relu("vector", h[closing[2]], h[closing[2]])
         diff(closing[3])
         finish(WIDE[2])
         for rows in ((0, 1), (2, 3)):
             output(LAST[0], rows)
             store(LAST[0], rows)
-        relu("vector", h[closing[3]], h[closing[3]])
         quantize_h(h[closing[2]], closing[2:3])
+        relu("vector", h[closing[3]], h[closing[3]])
         quantize_h(h[closing[3]], closing[3:])
         banks = [next_bank([P, 1, J]) for nt in range(4)]
         for b in range(2):

@@ -334,7 +334,7 @@ def tile_list_point_edge_conv_kernel(tc, tab_words, tab_scales, offs, offs2, off
         larger(turned[0])
         larger(turned[1])
         side(closing[0], 52)
-        larger(middle[0], 63.5)
+        larger(middle[0])
         centre(turned[0])
         larger(middle[1], 48)
         centre(turned[1])
@@ -345,19 +345,21 @@ def tile_list_point_edge_conv_kernel(tc, tab_words, tab_scales, offs, offs2, off
         wo_q = at(44.5, [P, 2, N], U32, "wo_q")
         nc.vector.quantize_mx(out=wo_q[:].rearrange("p b n -> p (b n)").bitcast(FP8X4), scales=wo_s[:].rearrange("p b n -> p (b n)"),
                               in_=wo_bf[:].rearrange("p b n -> p (b n)"))
-        h_wide = [at(kb, [P, 2048], BF16, "h_wide%d" % n) for n, kb in enumerate((60, 65, 1))]
+        h_open = keep.tile([P, 1024], BF16, align_bytes=64)
+        h_wide = [at(50.5, [P, 1024], BF16, "h_wide0"), at(53.5, [P, 2048], BF16, "h_wide1"), at(1, [P, 2048], BF16, "h_wide2")]
         place(h, h_wide[1][:, 1024:2048], turned)
-        relu("scalar", joined(h_wide[0][:, 1024:2048]), parted(d_open[:]))
+        relu("scalar", joined(h_open[:]), parted(d_open[:]))
         turn(turned[0])
         folded_second(folded[5])
-        side(closing[1], 54)
+        side(closing[1], 60)
         turn(turned[1])
         relu("scalar", joined(h_wide[2][:, 1024:2048]), parted(d_middle[:]))
-        side(closing[2], 56)
-        side(closing[3], 58)
+        side(closing[2], 62)
+        side(closing[3], 64)
         folded_max(h_wide[0], 0)
+        quantize_h(h_open[:], [(0, 1)], 52.5)
+        quantize_h(h_wide[0][:], [(0, 0)])
         folded_max(h_wide[1], 1)
-        quantize_h(h_wide[0][:], [(0, 0), (0, 1)])
         folded_max(h_wide[2], 2)
         quantize_h(h_wide[1][:], [(256, 0), (256, 1)])
         larger(closing[1])

from contextlib import ExitStack

import concourse.mybir as mybir
from concourse.masks import make_identity

K, T, S, H, N = 512, 2048, 1024, 1024, 512
FLOPS = 2 * (3 * K * H * S + H * N * S)

F32 = mybir.dt.float32
BF16 = mybir.dt.bfloat16
I32 = mybir.dt.int32
U32 = mybir.dt.uint32
U16 = mybir.dt.uint16
U8 = mybir.dt.uint8
FP8X4 = mybir.dt.float8_e4m3fn_x4
FP4X4 = mybir.dt.float4_e2m1fn_x4
ACT = mybir.ActivationFunctionType
ALU = mybir.AluOpType

P = 128
J = 128
KB = 1024
CENTRE, FIRST, SECOND = 0, 1, 2
F32_MAX = 3.4028234663852886e38

FOLD = 768
WIDE = ((0, 256), (256, 256), (512, 256))
LAST = ((768, 128), (896, 128))


def tile_list_point_edge_conv_kernel(tc, tab_words, tab_scales, offs, offs2, offs3, wc, wa_words, wa_scales,
                                                  wb_words, wb_scales, wo, bo, out):
    nc = tc.nc
    with ExitStack() as ctx:
        keep = ctx.enter_context(tc.tile_pool(name="keep", bufs=1))
        shared = ctx.enter_context(tc.tile_pool(name="shared", bufs=1))
        psum = ctx.enter_context(tc.psum_pool(name="psum", bufs=1))

        def at(kb, shape, dtype, name):
            return shared.tile(shape, dtype, name=name, align_bytes=64, offset=int(kb * KB))

        fills = []

        def next_bank(shape):
            fills.append(len(fills))
            return psum.tile(shape, F32, name="bank%d" % fills[-1], offset=2048 * (fills[-1] % 8))

        lists = [keep.tile([P, S // 16], U16, name="list%d" % i) for i in range(3)]
        tab_w = at(0, [P, T], I32, "tab_w")
        tab_s = keep.tile([P, T // 4], I32, align_bytes=64)
        wc_raw = [at((12, 36)[b], [P, 4, 512], F32, "wc_raw%d" % b) for b in range(2)]
        wc_bf = [at((20, 8)[b], [P, 2048], BF16, "wc_bf%d" % b) for b in range(2)]
        wc_q = keep.tile([P, H], U32, align_bytes=64)
        wc_s = keep.tile([P, H], U8, align_bytes=64)
        wb_raw = at(26, [P, H], I32, "wb_raw")
        wbs_raw = at(31, [P, H // 4], I32, "wbs_raw")
        wa_raw = keep.tile([P, H // 2], I32, align_bytes=64)
        was_raw = keep.tile([P, H // 4], I32, align_bytes=64)
        wa_q = keep.tile([P, H // 2], I32, align_bytes=64)
        wo_raw = [keep.tile([P, 4, N], F32, name="wo_raw%d" % b) for b in range(2)]
        wo_s = keep.tile([P, 2, N], U8, align_bytes=64)
        bias = keep.tile([P, 4], F32)
        res = keep.tile([P, 4, S], F32)

        def load_scales(dst, src):
            for q in range(4):
                nc.sync.dma_start(dst[32 * q : 32 * q + 4, :], src[0, 4 * q : 4 * q + 4, :].bitcast(I32))

        def load_wo(b):
            wo_rows = wo.rearrange("(b u t s) n -> b t u s n", b=2, t=4, s=4)
            for t in range(4):
                nc.sync.dma_start(wo_raw[b][:, t, :], wo_rows[b, t])

        nc.gpsimd.memset(tab_s[:], 0)
        nc.gpsimd.memset(was_raw[:], 0)
        nc.gpsimd.memset(wbs_raw[:], 0)
        identity = keep.tile([P, P], F32)
        make_identity(nc, identity[:])
        wc_rows = wc.rearrange("(p i) r -> p i r", i=4)
        nc.sync.dma_start(wa_raw[:], wa_words[0].bitcast(I32))
        nc.sync.dma_start(lists[FIRST][:], offs2)
        load_scales(tab_s, tab_scales)
        nc.sync.dma_start(lists[CENTRE][:], offs)
        nc.sync.dma_start(wc_raw[0][:], wc_rows[:, :, 0:512])
        nc.sync.dma_start(tab_w[:], tab_words[0].rearrange("p t i -> p (t i)").bitcast(I32))
        load_scales(was_raw, wa_scales)
        wb_rows = wb_words[0].rearrange("p e i -> p (e i)").bitcast(I32)
        for b in range(2):
            nc.sync.dma_start(wb_raw[:, 512 * b : 512 * (b + 1)], wb_rows[:, 512 * b : 512 * (b + 1)])
        nc.sync.dma_start(lists[SECOND][:], offs3)
        nc.sync.dma_start(wc_raw[1][:], wc_rows[:, :, 512:1024])
        load_scales(wbs_raw, wb_scales)
        load_wo(0)
        load_wo(1)
        with nc.allow_non_contiguous_dma(reason="one bias value a partition"):
            nc.sync.dma_start(bias[:], bo.rearrange("(t p) -> p t", p=P))

        got = {}

        def gather(window, dtype, i, first, count, dst):
            nc.vector.tensor_copy(dst[:], window[:].bitcast(dtype).indirect(lists[i][:, first // 16 : (first + count) // 16]))
            for j0 in range(first, first + count, J):
                got.setdefault((dtype == U32, i, j0), (dst, j0 - first))

        def picked(i, j0, n):
            (words, c0), (scales, d0) = got[True, i, j0], got[False, i, j0]
            return words[:, c0 : c0 + n].bitcast(FP8X4), scales[:, d0 : d0 + n]

        def vector_move(dst, src):
            nc.vector.tensor_copy(dst.bitcast(I32), src.bitcast(I32))

        def deal_columns(move, dst, src, run):
            move(dst.bitcast(U32).rearrange("p (b t u s) -> p b t u s", u=32, t=4, s=run),
                 src.bitcast(U32).rearrange("p (b u t s) -> p b t u s", u=32, t=4, s=run))

        def deal_scales(move, dst, src):
            move(dst[:].bitcast(U32).rearrange("p (b t g u) -> p b g t u", b=2, t=4, u=4),
                 src[:].bitcast(U32).rearrange("p (b g u t) -> p b g t u", b=2, t=4, u=4))

        def cast_wc(b):
            src = wc_raw[b][:].rearrange("p i (u t s) -> p t u i s", t=4, s=4)
            dst = wc_bf[b][:].rearrange("p (t u s i) -> p t u i s", t=4, s=4, i=4)
            for t in range(4):
                nc.scalar.activation(dst[:, t], src[:, t], ACT.Copy, scale=-1.0)

        def quantize_wc(b):
            nc.vector.quantize_mx(out=wc_q[:, 512 * b : 512 * (b + 1)].bitcast(FP8X4), scales=wc_s[:, 512 * b : 512 * (b + 1)], in_=wc_bf[b][:])

        def weights(i, col, n=P):
            if i == CENTRE:
                return wc_q[:, col : col + n].bitcast(FP8X4), wc_s[:, col : col + n]
            if i == FIRST:
                return wa_q[:].bitcast(U8)[:, 2 * col : 2 * (col + n)].bitcast(FP4X4), wa_s[:].bitcast(U8)[:, col : col + n]
            return wb_q[:, col : col + n].bitcast(FP8X4), wb_s[:].bitcast(U8)[:, col : col + n]

        def fill_bank(terms, unit):
            j0, b = unit[:2]
            slots, width = (range(4), J) if len(unit) == 2 else ((2 * unit[2], 2 * unit[2] + 1), 2 * J)
            bank = next_bank([P, len(slots), width])
            for e, t in enumerate(slots):
                for n, i in enumerate(terms):
                    w_codes, w_scales = weights(i, 512 * b + P * t)
                    v_codes, v_scales = picked(i, j0, width)
                    nc.tensor.matmul_mx(out=bank[:, e, :], lhsT=w_codes, lhsT_scale=w_scales, rhs=v_codes, rhs_scale=v_scales,
                                        start=(n == 0), stop=(n == len(terms) - 1))
            return bank[:].rearrange("p t j -> p j t")

        def fill_turned(i, unit):
            j0, b = unit
            bank = next_bank([P, 4 * P])
            w_codes, w_scales = weights(i, 512 * b, 512)
            v_codes, v_scales = picked(i, j0, J)
            nc.tensor.matmul_mx(out=bank[:], lhsT=v_codes, lhsT_scale=v_scales, rhs=w_codes, rhs_scale=w_scales, start=True, stop=True)
            return bank[:]

        def as_words(ap, unit):
            return ap.rearrange("p (j t) -> p j t", t=4 if len(unit) == 2 else 2)

        def joined(ap):
            return ap.rearrange("p (j g e) -> p j g e", g=2, e=2)

        def parted(ap):
            return ap.rearrange("p (g j e) -> p j g e", g=2, e=2)

        folded = [(j0, 0, g) for j0 in range(0, FOLD, 2 * J) for g in range(2)]
        opening = [(0, 1, 0), (0, 1, 1)]
        turned = [(256, 1), (384, 1)]
        middle = [(512, 1, 0), (512, 1, 1)]
        closing = [(j0, b) for j0 in (768, 896) for b in range(2)]
        sides, largers, centres, h, h_q = {}, {}, {}, {}, {}
        firsts, seconds = {}, {}

        def side(unit, kb):
            tile = at(kb, [P, 4 * J], F32, "side%d_%d" % (unit[0], sum(unit[1:])))
            if unit in turned:
                nc.scalar.activation(tile[:], fill_turned(FIRST, unit), ACT.Copy)
            else:
                nc.scalar.activation(as_words(tile[:], unit), fill_bank((FIRST,), unit), ACT.Copy)
            sides.setdefault(unit, tile)

        def folded_first(unit):
            nc.scalar.activation(as_words(firsts[unit], unit), fill_bank((FIRST, CENTRE), unit), ACT.Relu)

        def folded_second(unit):
            nc.scalar.activation(as_words(seconds[unit], unit), fill_bank((SECOND, CENTRE), unit), ACT.Copy)

        def larger(unit, kb=None):
            if kb is None:
                tile = keep.tile([P, 4 * J], F32, name="larger%d_%d" % (unit[0], sum(unit[1:])), align_bytes=64)
            else:
                tile = at(kb, [P, 4 * J], F32, "larger%d_%d" % (unit[0], sum(unit[1:])))
            if unit in turned:
                nc.vector.tensor_tensor(tile[:], fill_turned(SECOND, unit), sides[unit][:], ALU.max)
            else:
                nc.vector.tensor_tensor(as_words(tile[:], unit), fill_bank((SECOND,), unit), as_words(sides[unit][:], unit), ALU.max)
            largers.setdefault(unit, tile)

        def centre(unit):
            tile = keep.tile([P, 4 * P], F32, name="centre%d_%d" % (unit[0], sum(unit[1:])))
            nc.scalar.activation(tile[:], fill_turned(CENTRE, unit), ACT.Copy)
            centres.setdefault(unit, tile)

        def turn(unit):
            bank = next_bank([P, 4, J])
            for t in range(4):
                for n, term in enumerate((centres[unit], largers[unit])):
                    nc.tensor.matmul(bank[:, t, :], term[:, P * t : P * (t + 1)], identity[:], start=(n == 0), stop=(n == 1), is_transpose=True)
            nc.scalar.activation(as_words(h[unit], unit), bank[:].rearrange("p t j -> p j t"), ACT.Relu)

        def diff(unit):
            nc.vector.tensor_tensor(as_words(h[unit], unit), fill_bank((CENTRE,), unit), as_words(largers[unit][:], unit), ALU.add)

        def relu(engine, dst, src):
            if engine == "scalar":
                nc.scalar.activation(dst, src, ACT.Relu)
            elif engine == "gpsimd":
                nc.gpsimd.tensor_scalar(dst, src, F32_MAX, 0.0, ALU.min, ALU.max)
            else:
                nc.vector.tensor_scalar(dst, src, 0.0, None, ALU.max)

        def place(table, tile, units):
            for n, unit in enumerate(units):
                table.setdefault(unit, tile[:, 4 * J * n : 4 * J * (n + 1)])

        def folded_max(dst, n):
            cols = slice(1024 * n, 1024 * (n + 1))
            first = first_head[:] if n == 0 else first_rest[:, 1024 * (n - 1) : 1024 * n]
            nc.vector.tensor_tensor(joined(dst[:, 0:1024]), parted(second_bf[:, cols]), parted(first), ALU.max)

        def quantize_h(src, starts, kb=None):
            width = src.shape[1] // 4
            if kb is None:
                codes = keep.tile([P, width], U32, name="h_q%d_%d" % starts[0], align_bytes=64)
            else:
                codes = at(kb, [P, width], U32, "h_q%d_%d" % starts[0])
            scales = keep.tile([P, width], U8, name="h_s%d_%d" % starts[0], align_bytes=64)
            nc.vector.quantize_mx(out=codes[:].bitcast(FP8X4), scales=scales[:], in_=src)
            for n, start in enumerate(starts):
                h_q.setdefault(start, (codes, scales, width // len(starts) * n))

        out_rows = out.rearrange("(t p) j -> p t j", p=P)

        def second_layer(dst, nt, b, blk):
            j0, width = blk
            codes, scales, c0 = h_q[j0, b]
            nc.tensor.matmul_mx(out=dst, lhsT=wo_q[:, b, P * nt : P * (nt + 1)].bitcast(FP8X4), lhsT_scale=wo_s[:, b, P * nt : P * (nt + 1)],
                                rhs=codes[:, c0 : c0 + width].bitcast(FP8X4), rhs_scale=scales[:, c0 : c0 + width], start=(b == 0), stop=(b == 1))

        def read_out(bank, blk, rows, engine):
            cols = slice(blk[0], blk[0] + blk[1])
            for e, nt in enumerate(rows):
                if engine == "vector":
                    nc.vector.tensor_scalar(res[:, nt, cols], bank[:, e, :], bias[:, nt : nt + 1], 0.0, ALU.add, ALU.max)
                else:
                    nc.scalar.activation(res[:, nt, cols], bank[:, e, :], ACT.Relu, bias=bias[:, nt : nt + 1])

        def output(blk, rows, engine="scalar"):
            bank = next_bank([P, len(rows), blk[1]])
            for e, nt in enumerate(rows):
                for b in range(2):
                    second_layer(bank[:, e, :], nt, b, blk)
            read_out(bank, blk, rows, engine)

        def half_pass(banks, blk, b):
            for nt in range(4):
                second_layer(banks[nt][:, 0, :], nt, b, blk)

        def store(blk, rows):
            cols = slice(blk[0], blk[0] + blk[1])
            nc.sync.dma_start(out_rows[:, rows[0] : rows[-1] + 1, cols], res[:, rows[0] : rows[-1] + 1, cols])

        def finish(blk):
            for rows in ((0, 1), (2, 3)) if blk[1] == 256 else ((0, 1, 2, 3),):
                output(blk, rows)
                store(blk, rows)

        deal_columns(vector_move, wa_q[:], wa_raw[:], 2)
        gather(tab_s, U8, FIRST, 0, S, keep.tile([P, S], U8, name="got_s1", align_bytes=64))
        gather(tab_s, U8, CENTRE, 0, S, keep.tile([P, S], U8, name="got_s0", align_bytes=64))
        gather(tab_w, U32, FIRST, 0, 256, keep.tile([P, 256], U32, name="got_w1_head", align_bytes=64))
        cast_wc(0)
        wa_s = keep.tile([P, H // 4], I32, align_bytes=64)
        wb_s = keep.tile([P, H // 4], I32, align_bytes=64)
        wb_q = keep.tile([P, H], I32, align_bytes=64)
        deal_scales(nc.scalar.copy, wa_s, was_raw)
        for b in range(2):
            deal_columns(nc.scalar.copy, wb_q[:, 512 * b : 512 * (b + 1)], wb_raw[:, 512 * b : 512 * (b + 1)], 4)
        quantize_wc(0)
        gather(tab_w, U32, CENTRE, 0, 256, at(12, [P, 256], U32, "got_w0_head"))
        gather(tab_w, U32, FIRST, 256, 768, at(20, [P, 768], U32, "got_w1_rest"))
        gather(tab_w, U32, CENTRE, 256, 512, at(23, [P, 512], U32, "got_w0_mid"))
        gather(tab_s, U8, SECOND, 0, S, keep.tile([P, S], U8, name="got_s2", align_bytes=64))
        gather(tab_w, U32, SECOND, 0, 512, keep.tile([P, 512], U32, name="got_w2_head", align_bytes=64))
        first_head = at(25, [P, 1024], BF16, "first_head")
        place(firsts, first_head, folded[:2])
        side(opening[0], 27)
        side(opening[1], 29)
        folded_first(folded[0])
        folded_first(folded[1])
        cast_wc(1)
        deal_scales(nc.scalar.copy, wb_s, wbs_raw)
        quantize_wc(1)
        gather(tab_w, U32, CENTRE, 768, 256, at(31, [P, 256], U32, "got_w0_rest"))
        gather(tab_w, U32, SECOND, 512, 512, keep.tile([P, 512], U32, name="got_w2_rest", align_bytes=64))
        wo_bf = at(1, [P, 2, 4 * N], BF16, "wo_bf")
        for b in range(2):
            nc.gpsimd.tensor_scalar(wo_bf[:, b, :].rearrange("p (n t) -> p n t", t=4), wo_raw[b][:].rearrange("p t n -> p n t"),
                                    1.0, 0.0, ALU.mult, ALU.add)
        d_open = keep.tile([P, 1024], BF16, align_bytes=64)
        d_middle = keep.tile([P, 1024], BF16, align_bytes=64)
        h_last = [keep.tile([P, 1024], BF16, name="h_last%d" % n, align_bytes=64) for n in range(2)]
        place(h, d_open, opening)
        place(h, d_middle, middle)
        place(h, h_last[0], closing[:2])
        place(h, h_last[1], closing[2:])
        first_rest = at(32.5, [P, 2048], BF16, "first_rest")
        place(firsts, first_rest, folded[2:])
        second_bf = keep.tile([P, 3072], BF16, align_bytes=64)
        place(seconds, second_bf, folded)
        side(turned[0], 36.5)
        side(turned[1], 38.5)
        for unit in folded[2:]:
            folded_first(unit)
        side(middle[0], 40.5)
        side(middle[1], 42.5)
        folded_second(folded[0])
        larger(opening[0])
        larger(opening[1])
        folded_second(folded[1])
        diff(opening[0])
        folded_second(folded[2])
        diff(opening[1])
        folded_second(folded[3])
        larger(turned[0])
        larger(turned[1])
        side(closing[0], 52)
        larger(middle[0])
        centre(turned[0])
        larger(middle[1], 48)
        centre(turned[1])
        diff(middle[0])
        folded_second(folded[4])
        diff(middle[1])
        larger(closing[0])
        wo_q = at(44.5, [P, 2, N], U32, "wo_q")
        nc.vector.quantize_mx(out=wo_q[:].rearrange("p b n -> p (b n)").bitcast(FP8X4), scales=wo_s[:].rearrange("p b n -> p (b n)"),
                              in_=wo_bf[:].rearrange("p b n -> p (b n)"))
        h_open = keep.tile([P, 1024], BF16, align_bytes=64)
        h_wide = [at(50.5, [P, 1024], BF16, "h_wide0"), at(53.5, [P, 2048], BF16, "h_wide1"), at(1, [P, 2048], BF16, "h_wide2")]
        place(h, h_wide[1][:, 1024:2048], turned)
        relu("scalar", joined(h_open[:]), parted(d_open[:]))
        turn(turned[0])
        folded_second(folded[5])
        side(closing[1], 60)
        turn(turned[1])
        relu("scalar", joined(h_wide[2][:, 1024:2048]), parted(d_middle[:]))
        side(closing[2], 62)
        side(closing[3], 64)
        folded_max(h_wide[0], 0)
        quantize_h(h_open[:], [(0, 1)], 52.5)
        quantize_h(h_wide[0][:], [(0, 0)])
        folded_max(h_wide[1], 1)
        folded_max(h_wide[2], 2)
        quantize_h(h_wide[1][:], [(256, 0), (256, 1)])
        larger(closing[1])
        quantize_h(h_wide[2][:], [(512, 0), (512, 1)])
        diff(closing[0])
        diff(closing[1])
        finish(WIDE[0])
        relu("gpsimd", h[closing[0]], h[closing[0]])
        relu("gpsimd", h[closing[1]], h[closing[1]])
        larger(closing[2])
        finish(WIDE[1])
        larger(closing[3])
        diff(closing[2])
        quantize_h(h_last[0][:], closing[:2])
        relu("vector", h[closing[2]], h[closing[2]])
        diff(closing[3])
        finish(WIDE[2])
        for rows in ((0, 1), (2, 3)):
            output(LAST[0], rows)
            store(LAST[0], rows)
        quantize_h(h[closing[2]], closing[2:3])
        relu("vector", h[closing[3]], h[closing[3]])
        quantize_h(h[closing[3]], closing[3:])
        banks = [next_bank([P, 1, J]) for nt in range(4)]
        for b in range(2):
            half_pass(banks, LAST[1], b)
        for nt in range(4):
            read_out(banks[nt], LAST[1], (nt,), ("vector", "scalar")[nt % 2])
            if nt % 2:
                store(LAST[1], (nt - 1, nt))
